import numpy as np
import ml_dtypes


def mxq(x, axis, fmt="e4m3"):
    dtype, down = {"e4m3": (ml_dtypes.float8_e4m3fn, 7), "e5m2": (ml_dtypes.float8_e5m2, 14)}[fmt]
    v = np.moveaxis(np.asarray(x, np.float32).astype(ml_dtypes.bfloat16).astype(np.float64), axis, -1)
    blocks = v.reshape(v.shape[:-1] + (-1, 32))
    amax = np.abs(blocks).max(-1, keepdims=True)
    byte = np.maximum(np.where(amax > 0, np.frexp(amax)[1] - 1 + 127, 0) - down, 1)
    scale = np.exp2(byte - 127.0)
    codes = (blocks / scale).astype(np.float32).astype(dtype).astype(np.float64)
    return np.moveaxis((codes * scale).reshape(v.shape), -1, axis)


WIDE = False


def mx_kscale(k, group=512):
    if not WIDE:
        return np.ones(k)
    levels = np.array([10, -10, 5, -5, 0])
    if group != 512:
        return np.exp2(np.random.permutation(np.resize(levels, k // group))).repeat(group)
    if k % 512:
        return np.exp2(np.random.permutation(np.resize(levels, k // 32))).repeat(32)
    a = np.empty((k // 512, 16))
    for p in range(k // 512):
        a[p, :8] = np.random.permutation(np.resize(levels, 8))
        for g in range(8):
            far = levels[np.abs(levels - a[p, g]) >= 10]
            a[p, g + 8] = far[np.random.randint(len(far))]
    return np.exp2(a.ravel()).repeat(32)


def f64(x):
    return np.asarray(x).astype(np.float64)


def striped(idx):
    return np.tile(np.asarray(idx).reshape(-1, 16).T, (8, 1)).astype(np.uint16)


def unstriped(offs):
    return offs[:16].T.reshape(-1).astype(np.int64)


H, KV, D, NQ, N = 2, 2, 256, 512, 512
CAP = 2.0


def setup_inputs():
    n = np.random.standard_normal
    s = mx_kscale(D, 0)[:, None]
    u = mx_kscale(N)
    t = np.random.uniform(0.5, 2.0, N) * u
    v = n((KV, N, 128))
    v[:, :, 127] = 1.0
    return {
        "qT": (n((H, D, NQ)) * s * (0.70 / np.sqrt(D))).astype(np.float32),
        "kT": (n((KV, D, N)) / s).astype(np.float32),
        "t": t.reshape(N, 1).astype(np.float32),
        "v": (v / t[:, None]).astype(np.float32),
        "kb": (0.5 * n((N, 1))).astype(np.float32),
    }


def reference(qT, kT, t, v, kb):
    a = mxq(f64(kT), 1, "e4m3").transpose(0, 2, 1) @ mxq(f64(qT), 1, "e4m3")
    a = a + f64(kb)
    a = CAP * np.tanh(a / CAP)
    p = np.square(np.maximum(a, 0.0))
    w = p * f64(t)
    y = mxq(w, 1, "e4m3").transpose(0, 2, 1) @ mxq(f64(v), 1, "e4m3")
    y = y / (y[:, :, 127:128] + 1.0)
    return y

@@ -1,0 +1,187 @@
+from contextlib import ExitStack
+
+import concourse.mybir as mybir
+
+F32 = mybir.dt.float32
+BF16 = mybir.dt.bfloat16
+U32 = mybir.dt.uint32
+U8 = mybir.dt.uint8
+FP8X4 = mybir.dt.float8_e4m3fn_x4
+ACT = mybir.ActivationFunctionType
+ALU = mybir.AluOpType
+
+H, D, NQ, N, E = 2, 256, 512, 512, 128
+P = 128
+FLOPS = 2 * H * NQ * N * (D + E)
+RUN = 4
+USEPOW = False
+ORDER = [('abs', 'V'), ('root', 'S'), ('ck00', 'S'), ('ck01', 'V'), ('ck11', 'V'), ('qk20', 'V'), ('qk00', 'V'), ('qk10', 'V'), ('sign', 'S'), ('cq1', 'V'), ('cq0', 'V'), ('qq1', 'V'), ('ck10', 'S'), ('qk11', 'V'), ('qk21', 'V'), ('qq0', 'V'), ('mm112', 'P'), ('mm012', 'P'), ('mm111', 'P'), ('mm011', 'P'), ('mm002', 'P'), ('qk31', 'V'), ('qk01', 'V'), ('mm102', 'P'), ('prepk', 'V'), ('T012', 'S'), ('qk30', 'V'), ('cq3', 'V'), ('cq2', 'V'), ('mm101', 'P'), ('T011', 'S'), ('mm000', 'P'), ('mm001', 'P'), ('mm113', 'P'), ('cv1', 'V'), ('T002', 'S'), ('T001', 'S'), ('mm013', 'P'), ('qq2', 'V'), ('mm100', 'P'), ('A011', 'V'), ('mm010', 'P'), ('mm110', 'P'), ('T013', 'S'), ('A012', 'V'), ('mm103', 'P'), ('mm003', 'P'), ('T000', 'S'), ('T010', 'S'), ('mm301', 'P'), ('A002', 'V'), ('mm303', 'P'), ('qv1', 'V'), ('mm201', 'P'), ('T003', 'S'), ('mm203', 'P'), ('T203', 'S'), ('mm313', 'P'), ('A001', 'V'), ('mm202', 'P'), ('cv0', 'V'), ('A013', 'V'), ('A010', 'V'), ('A000', 'V'), ('A003', 'V'), ('mm300', 'P'), ('B01', 'V'), ('T201', 'S'), ('A203', 'V'), ('mm212', 'P'), ('mm302', 'P'), ('T202', 'S'), ('A201', 'V'), ('mm210', 'P'), ('Q01', 'V'), ('mm310', 'P'), ('mm312', 'P'), ('B10', 'S'), ('mm213', 'P'), ('qv0', 'V'), ('A202', 'V'), ('mm211', 'P'), ('B11', 'V'), ('mm311', 'P'), ('T213', 'S'), ('mm200', 'P'), ('T200', 'S'), ('Q10', 'V'), ('y01', 'P'), ('A200', 'V'), ('T212', 'S'), ('Q11', 'V'), ('A213', 'V'), ('T210', 'S'), ('y10', 'P'), ('A212', 'V'), ('y11', 'P'), ('T211', 'S'), ('B00', 'S'), ('den0111', 'S'), ('B20', 'V'), ('B30', 'S'), ('A211', 'V'), ('A210', 'V'), ('B21', 'S'), ('Q20', 'V'), ('Q00', 'V'), ('y20', 'P'), ('den20', 'S'), ('y00', 'P'), ('rc0111', 'V'), ('B31', 'V'), ('Q30', 'V'), ('den0010', 'V'), ('E0111', 'S'), ('Q31', 'V'), ('Q21', 'V'), ('y30', 'P'), ('rc20', 'V'), ('y31', 'P'), ('den31', 'S'), ('rc0010', 'V'), ('y21', 'P'), ('den21', 'S'), ('st0111', 'Y'), ('den30', 'V'), ('E0010', 'V'), ('st0010', 'Y'), ('rc30', 'V'), ('rc31', 'V'), ('E20', 'S'), ('st20', 'Y'), ('rc21', 'V'), ('E30', 'S'), ('st30', 'Y'), ('E31', 'V'), ('st31', 'Y'), ('E21', 'V'), ('st21', 'Y')]
+YSLOT = {(0, 0): (5, 0), (1, 0): (5, 1), (0, 1): (6, 0), (1, 1): (6, 1), (2, 0): (7, 0), (3, 0): (5, 2), (2, 1): (6, 2), (3, 1): (7, 1)}
+SBANK = {(0, 0, 0): (0, 0), (0, 0, 1): (1, 0), (0, 0, 2): (2, 0), (0, 0, 3): (2, 2), (0, 1, 0): (3, 0), (0, 1, 1): (3, 2), (0, 1, 2): (4, 0), (0, 1, 3): (4, 2), (2, 0, 0): (0, 2), (2, 0, 1): (1, 2), (2, 0, 2): (0, 0), (2, 0, 3): (1, 0), (2, 1, 0): (3, 0), (2, 1, 1): (3, 2), (2, 1, 2): (4, 0), (2, 1, 3): (4, 2)}
+QQ = {0: 1, 1: 1, 2: 2}
+
+
+def tile_rows_a_relu2_kb_cap_kernel(tc, qT, kT, t, v, kb, out):
+    nc = tc.nc
+    with ExitStack() as ctx:
+        sb = ctx.enter_context(tc.tile_pool(name="sb", bufs=1))
+        ps = ctx.enter_context(tc.psum_pool(name="ps", bufs=1))
+
+        def tile(shape, dtype, name):
+            return sb.tile(shape, dtype, name=name, align_bytes=64)
+
+        banks = [ps.tile([P, 512], F32, name="bank%d" % b) for b in range(8)]
+        t_raw = tile([P, 4], F32, "t_raw")
+        kb_raw = tile([P, 4], F32, "kb_raw")
+        t_abs = tile([P, 4], F32, "t_abs")
+        t_pow = tile([P, 4], F32, "t_pow")
+        half = tile([P, 4], F32, "half")
+        root = tile([P, 4], F32, "root")
+        sign = tile([P, 4], F32, "sign")
+        kb_half = tile([P, 4], F32, "kb_half")
+        k_raw = [tile([P, 4, 256], F32, "k_raw%d" % m) for m in range(2)]
+        q_raw = [tile([P, 4, 256], F32, "q_raw%d" % m) for m in range(2)]
+        v_raw = [tile([P, 4, E], F32, "v_raw%d" % h) for h in range(H)]
+        k_bf = tile([P, 4, 128, 4], BF16, "k_bf")
+        q_bf = tile([P, NQ, 4], BF16, "q_bf")
+        v_bf = tile([P, H, E, 4], BF16, "v_bf")
+        k_c = tile([P, 4, 128], U32, "k_c")
+        k_s = tile([P, 4, 128], U8, "k_s")
+        q_c = tile([P, NQ], U32, "q_c")
+        q_s = tile([P, NQ], U8, "q_s")
+        v_c = tile([P, H, E], U32, "v_c")
+        v_s = tile([P, H, E], U8, "v_s")
+        th = {(g, h): tile([P, 4, 256], F32, "th%d%d" % (g, h)) for g in range(2) for h in range(H)}
+        u = {(g, h): tile([P, 4, 256], F32, "u%d%d" % (g, h)) for g in range(2) for h in range(H)}
+        w_bf = {(c, h): tile([P, 128, 4], BF16, "w_bf%d%d" % (c, h)) for c in range(4) for h in range(H)}
+        w_c = {(c, h): tile([P, 128], U32, "w_c%d%d" % (c, h)) for c in range(4) for h in range(H)}
+        w_s = {(c, h): tile([P, 128], U8, "w_s%d%d" % (c, h)) for c in range(4) for h in range(H)}
+        den, rec, res = {}, {}, {}
+
+        kv = kT.rearrange("h (p j) n -> (h p) j n", j=4)
+        qv = qT.rearrange("h (p j) n -> (h p) j n", j=4)
+
+        def copy(eng, out, in_):
+            if eng == "V":
+                nc.vector.tensor_copy(out=out, in_=in_)
+            else:
+                nc.scalar.copy(out=out, in_=in_)
+
+        def units(s):
+            return [(int(s[i]), int(s[i + 1])) for i in range(0, len(s), 2)]
+
+        def yview(us):
+            b, s = YSLOT[us[0]]
+            return banks[b][:, 128 * s : 128 * (s + len(us))].rearrange("p (n e) -> p n e", e=E)
+
+        ctx.enter_context(tc.manual_schedule())
+        nc.scalar.dma_start(out=t_raw[:], in_=t.rearrange("(p r) o -> p (r o)", r=4))
+        nc.sync.dma_start(out=k_raw[0][:], in_=kv[:, :, 0:256])
+        nc.sync.dma_start(out=k_raw[1][:], in_=kv[:, :, 256:512])
+        nc.sync.dma_start(out=q_raw[0][:], in_=qv[:, :, 0:256])
+        nc.sync.dma_start(out=kb_raw[:], in_=kb.rearrange("(p r) o -> p (r o)", r=4))
+        nc.sync.dma_start(out=q_raw[1][:], in_=qv[:, :, 256:512])
+        for h in range(H):
+            nc.sync.dma_start(out=v_raw[h][:], in_=v[h].rearrange("(p j) e -> p j e", j=4))
+        if USEPOW:
+            nc.gpsimd.memset(half[:], 0.5)
+
+        for name, eng in ORDER:
+            if name == "abs":
+                nc.vector.scalar_tensor_tensor(out=t_abs[:], in0=t_raw[:], scalar=-1.0, in1=t_raw[:], op0=ALU.mult, op1=ALU.max)
+            elif name == "pow":
+                nc.gpsimd.tensor_tensor(out=t_pow[:], in0=t_abs[:], in1=half[:], op=ALU.pow)
+            elif name == "root":
+                if USEPOW:
+                    nc.scalar.activation(out=root[:], in_=t_pow[:], func=ACT.Copy, scale=2.0)
+                else:
+                    nc.scalar.activation(out=root[:], in_=t_abs[:], func=ACT.Sqrt, scale=4.0)
+            elif name == "sign":
+                nc.scalar.activation(out=sign[:], in_=t_raw[:], func=ACT.Sign)
+            elif name == "prepk":
+                nc.vector.tensor_scalar_mul(out=kb_half[:], in0=kb_raw[:], scalar1=0.5)
+            elif name.startswith("ck"):
+                m, i = int(name[2]), int(name[3])
+                s0 = 64 * m + 32 * i
+                copy(eng, k_bf[:, :, s0 : s0 + 32, :].rearrange("p r s j -> p s j r"),
+                     k_raw[m][:, :, 128 * i : 128 * i + 128].rearrange("p j (s r) -> p s j r", r=4))
+            elif name.startswith("qk"):
+                r, m = int(name[2]), int(name[3])
+                nc.vector.quantize_mx(out=k_c[:, r, 64 * m : 64 * m + 64].bitcast(FP8X4), scales=k_s[:, r, 64 * m : 64 * m + 64],
+                                      in_=k_bf[:, r, 64 * m : 64 * m + 64, :].rearrange("p s j -> p (s j)"))
+            elif name.startswith("cq"):
+                c = int(name[2])
+                copy(eng, q_bf[:, 128 * c : 128 * c + 128, :].rearrange("p (n i) j -> p n j i", i=RUN),
+                     q_raw[c // 2][:, :, 128 * (c % 2) : 128 * (c % 2) + 128].rearrange("p j (n i) -> p n j i", i=RUN))
+            elif name.startswith("qq"):
+                c = int(name[2])
+                cols = slice(128 * c, 128 * (c + QQ[c]))
+                nc.vector.quantize_mx(out=q_c[:, cols].bitcast(FP8X4), scales=q_s[:, cols], in_=q_bf[:, cols, :].rearrange("p n j -> p (n j)"))
+            elif name.startswith("cv"):
+                h = int(name[2])
+                nc.vector.tensor_tensor(out=v_bf[:, h, :, :].rearrange("p (n i) j -> p n j i", i=RUN),
+                                        in0=v_raw[h][:].rearrange("p j (n i) -> p n j i", i=RUN),
+                                        in1=sign[:].unsqueeze(1).unsqueeze(3).to_broadcast([P, E // RUN, 4, RUN]), op=ALU.mult)
+            elif name.startswith("qv"):
+                h = int(name[2])
+                nc.vector.quantize_mx(out=v_c[:, h, :].bitcast(FP8X4), scales=v_s[:, h, :], in_=v_bf[:, h, :, :].rearrange("p e j -> p (e j)"))
+            elif name.startswith("mm"):
+                c, h, r = int(name[2]), int(name[3]), int(name[4])
+                b, s = SBANK[(2 * (c // 2), h, r)]
+                s += c % 2
+                rows = slice(64 * h, 64 * h + 64)
+                cols = slice(128 * c, 128 * c + 128)
+                nc.tensor.matmul_mx(out=banks[b][:, 128 * s : 128 * s + 128], lhsT=k_c[rows, r, :].bitcast(FP8X4), lhsT_scale=k_s[rows, r, :],
+                                    rhs=q_c[rows, cols].bitcast(FP8X4), rhs_scale=q_s[rows, cols], start=True, stop=True)
+            elif name[0] == "T":
+                c, h, r = int(name[1]), int(name[2]), int(name[3])
+                b, s = SBANK[(c, h, r)]
+                nc.scalar.activation(out=th[(c // 2, h)][:, r, :], in_=banks[b][:, 128 * s : 128 * s + 256], func=ACT.Tanh,
+                                     bias=kb_half[:, r : r + 1], scale=0.5)
+            elif name[0] == "A":
+                c, h, r = int(name[1]), int(name[2]), int(name[3])
+                nc.vector.tensor_scalar(out=u[(c // 2, h)][:, r, :], in0=th[(c // 2, h)][:, r, :], scalar1=0.0, scalar2=root[:, r : r + 1],
+                                        op0=ALU.max, op1=ALU.mult)
+            elif name[0] == "B":
+                c, h = int(name[1]), int(name[2])
+                src = u[(c // 2, h)][:, :, 128 * (c % 2) : 128 * (c % 2) + 128].rearrange("p r (n i) -> p n r i", i=RUN)
+                dst = w_bf[(c, h)][:].rearrange("p (n i) r -> p n r i", i=RUN)
+                if eng == "V":
+                    nc.vector.tensor_tensor(out=dst, in0=src, in1=src, op=ALU.mult)
+                else:
+                    nc.scalar.activation(out=dst, in_=src, func=ACT.Square)
+            elif name[0] == "Q":
+                c, h = int(name[1]), int(name[2])
+                nc.vector.quantize_mx(out=w_c[(c, h)][:].bitcast(FP8X4), scales=w_s[(c, h)][:], in_=w_bf[(c, h)][:].rearrange("p n r -> p (n r)"))
+            elif name[0] == "y":
+                c, h = int(name[1]), int(name[2])
+                b, s = YSLOT[(c, h)]
+                nc.tensor.matmul_mx(out=banks[b][:, 128 * s : 128 * s + 128], lhsT=w_c[(c, h)][:].bitcast(FP8X4), lhsT_scale=w_s[(c, h)][:],
+                                    rhs=v_c[:, h, :].bitcast(FP8X4), rhs_scale=v_s[:, h, :], start=True, stop=True)
+            elif name.startswith("den"):
+                key = name[3:]
+                us = units(key)
+                den[key] = tile([P, len(us)], F32, "den" + key)
+                src = yview(us)[:, :, E - 1]
+                if eng == "V":
+                    nc.vector.tensor_scalar_add(out=den[key][:], in0=src, scalar1=1.0)
+                else:
+                    nc.scalar.activation(out=den[key][:], in_=src, func=ACT.Copy, bias=1.0)
+            elif name.startswith("rc"):
+                key = name[2:]
+                rec[key] = tile([P, len(key) // 2], F32, "rec" + key)
+                nc.vector.reciprocal(out=rec[key][:], in_=den[key][:])
+            elif name[0] == "E":
+                key = name[1:]
+                us = units(key)
+                res[key] = tile([P, len(us), E], F32, "res" + key)
+                if eng == "V":
+                    nc.vector.tensor_tensor(out=res[key][:], in0=yview(us), in1=rec[key][:].unsqueeze(2).to_broadcast([P, len(us), E]), op=ALU.mult)
+                else:
+                    for i in range(len(us)):
+                        nc.scalar.activation(out=res[key][:, i, :], in_=yview(us)[:, i, :], func=ACT.Copy, scale=rec[key][:, i : i + 1])
+            elif name.startswith("st"):
+                key = name[2:]
+                us = units(key)
+                c, h = us[0]
+                nc.sync.dma_start(out=out[h, 128 * c : 128 * (c + len(us)), :].rearrange("(n p) e -> p n e", p=P), in_=res[key][:])

@@ -11,177 +11,280 @@ ACT = mybir.ActivationFunctionType
 ALU = mybir.AluOpType
 
 H, D, NQ, N, E = 2, 256, 512, 512, 128
-P = 128
 FLOPS = 2 * H * NQ * N * (D + E)
+
+P = 128
+PACK = 4
+ROWS = D // PACK
+QB = 128
+HALF = N // 2
 RUN = 4
-USEPOW = False
-ORDER = [('abs', 'V'), ('root', 'S'), ('ck00', 'S'), ('ck01', 'V'), ('ck11', 'V'), ('qk20', 'V'), ('qk00', 'V'), ('qk10', 'V'), ('sign', 'S'), ('cq1', 'V'), ('cq0', 'V'), ('qq1', 'V'), ('ck10', 'S'), ('qk11', 'V'), ('qk21', 'V'), ('qq0', 'V'), ('mm112', 'P'), ('mm012', 'P'), ('mm111', 'P'), ('mm011', 'P'), ('mm002', 'P'), ('qk31', 'V'), ('qk01', 'V'), ('mm102', 'P'), ('prepk', 'V'), ('T012', 'S'), ('qk30', 'V'), ('cq3', 'V'), ('cq2', 'V'), ('mm101', 'P'), ('T011', 'S'), ('mm000', 'P'), ('mm001', 'P'), ('mm113', 'P'), ('cv1', 'V'), ('T002', 'S'), ('T001', 'S'), ('mm013', 'P'), ('qq2', 'V'), ('mm100', 'P'), ('A011', 'V'), ('mm010', 'P'), ('mm110', 'P'), ('T013', 'S'), ('A012', 'V'), ('mm103', 'P'), ('mm003', 'P'), ('T000', 'S'), ('T010', 'S'), ('mm301', 'P'), ('A002', 'V'), ('mm303', 'P'), ('qv1', 'V'), ('mm201', 'P'), ('T003', 'S'), ('mm203', 'P'), ('T203', 'S'), ('mm313', 'P'), ('A001', 'V'), ('mm202', 'P'), ('cv0', 'V'), ('A013', 'V'), ('A010', 'V'), ('A000', 'V'), ('A003', 'V'), ('mm300', 'P'), ('B01', 'V'), ('T201', 'S'), ('A203', 'V'), ('mm212', 'P'), ('mm302', 'P'), ('T202', 'S'), ('A201', 'V'), ('mm210', 'P'), ('Q01', 'V'), ('mm310', 'P'), ('mm312', 'P'), ('B10', 'S'), ('mm213', 'P'), ('qv0', 'V'), ('A202', 'V'), ('mm211', 'P'), ('B11', 'V'), ('mm311', 'P'), ('T213', 'S'), ('mm200', 'P'), ('T200', 'S'), ('Q10', 'V'), ('y01', 'P'), ('A200', 'V'), ('T212', 'S'), ('Q11', 'V'), ('A213', 'V'), ('T210', 'S'), ('y10', 'P'), ('A212', 'V'), ('y11', 'P'), ('T211', 'S'), ('B00', 'S'), ('den0111', 'S'), ('B20', 'V'), ('B30', 'S'), ('A211', 'V'), ('A210', 'V'), ('B21', 'S'), ('Q20', 'V'), ('Q00', 'V'), ('y20', 'P'), ('den20', 'S'), ('y00', 'P'), ('rc0111', 'V'), ('B31', 'V'), ('Q30', 'V'), ('den0010', 'V'), ('E0111', 'S'), ('Q31', 'V'), ('Q21', 'V'), ('y30', 'P'), ('rc20', 'V'), ('y31', 'P'), ('den31', 'S'), ('rc0010', 'V'), ('y21', 'P'), ('den21', 'S'), ('st0111', 'Y'), ('den30', 'V'), ('E0010', 'V'), ('st0010', 'Y'), ('rc30', 'V'), ('rc31', 'V'), ('E20', 'S'), ('st20', 'Y'), ('rc21', 'V'), ('E30', 'S'), ('st30', 'Y'), ('E31', 'V'), ('st31', 'Y'), ('E21', 'V'), ('st21', 'Y')]
-YSLOT = {(0, 0): (5, 0), (1, 0): (5, 1), (0, 1): (6, 0), (1, 1): (6, 1), (2, 0): (7, 0), (3, 0): (5, 2), (2, 1): (6, 2), (3, 1): (7, 1)}
-SBANK = {(0, 0, 0): (0, 0), (0, 0, 1): (1, 0), (0, 0, 2): (2, 0), (0, 0, 3): (2, 2), (0, 1, 0): (3, 0), (0, 1, 1): (3, 2), (0, 1, 2): (4, 0), (0, 1, 3): (4, 2), (2, 0, 0): (0, 2), (2, 0, 1): (1, 2), (2, 0, 2): (0, 0), (2, 0, 3): (1, 0), (2, 1, 0): (3, 0), (2, 1, 1): (3, 2), (2, 1, 2): (4, 0), (2, 1, 3): (4, 2)}
-QQ = {0: 1, 1: 1, 2: 2}
+
+GROUPS = [(0, 1), (1, 1), (2, 2)]
+STEPS = [(g, r) for g in range(len(GROUPS)) for r in range(PACK)]
+SCORE_BANKS = 3
+Y_PLACE = {(0, 0): (0, 0), (1, 0): (0, 1), (2, 0): (0, 2), (3, 1): (0, 3),
+           (0, 1): (1, 0), (1, 1): (1, 1), (3, 0): (1, 2), (2, 1): (1, 3)}
 
 
 def tile_rows_a_relu2_kb_cap_kernel(tc, qT, kT, t, v, kb, out):
     nc = tc.nc
     with ExitStack() as ctx:
-        sb = ctx.enter_context(tc.tile_pool(name="sb", bufs=1))
-        ps = ctx.enter_context(tc.psum_pool(name="ps", bufs=1))
+        sbuf = ctx.enter_context(tc.tile_pool(name="sbuf", bufs=1))
+        psum = ctx.enter_context(tc.psum_pool(name="psum", bufs=1))
 
-        def tile(shape, dtype, name):
-            return sb.tile(shape, dtype, name=name, align_bytes=64)
+        def tile(name, shape, dtype):
+            return sbuf.tile(shape, dtype, name=name, align_bytes=64)
 
-        banks = [ps.tile([P, 512], F32, name="bank%d" % b) for b in range(8)]
-        t_raw = tile([P, 4], F32, "t_raw")
-        kb_raw = tile([P, 4], F32, "kb_raw")
-        t_abs = tile([P, 4], F32, "t_abs")
-        t_pow = tile([P, 4], F32, "t_pow")
-        half = tile([P, 4], F32, "half")
-        root = tile([P, 4], F32, "root")
-        sign = tile([P, 4], F32, "sign")
-        kb_half = tile([P, 4], F32, "kb_half")
-        k_raw = [tile([P, 4, 256], F32, "k_raw%d" % m) for m in range(2)]
-        q_raw = [tile([P, 4, 256], F32, "q_raw%d" % m) for m in range(2)]
-        v_raw = [tile([P, 4, E], F32, "v_raw%d" % h) for h in range(H)]
-        k_bf = tile([P, 4, 128, 4], BF16, "k_bf")
-        q_bf = tile([P, NQ, 4], BF16, "q_bf")
-        v_bf = tile([P, H, E, 4], BF16, "v_bf")
-        k_c = tile([P, 4, 128], U32, "k_c")
-        k_s = tile([P, 4, 128], U8, "k_s")
-        q_c = tile([P, NQ], U32, "q_c")
-        q_s = tile([P, NQ], U8, "q_s")
-        v_c = tile([P, H, E], U32, "v_c")
-        v_s = tile([P, H, E], U8, "v_s")
-        th = {(g, h): tile([P, 4, 256], F32, "th%d%d" % (g, h)) for g in range(2) for h in range(H)}
-        u = {(g, h): tile([P, 4, 256], F32, "u%d%d" % (g, h)) for g in range(2) for h in range(H)}
-        w_bf = {(c, h): tile([P, 128, 4], BF16, "w_bf%d%d" % (c, h)) for c in range(4) for h in range(H)}
-        w_c = {(c, h): tile([P, 128], U32, "w_c%d%d" % (c, h)) for c in range(4) for h in range(H)}
-        w_s = {(c, h): tile([P, 128], U8, "w_s%d%d" % (c, h)) for c in range(4) for h in range(H)}
-        den, rec, res = {}, {}, {}
+        score_bank = [[psum.tile([P, 512], F32, name="score%d%d" % (h, b)) for b in range(SCORE_BANKS)] for h in range(H)]
+        y_bank = [psum.tile([P, 4, E], F32, name="y%d" % b) for b in range(2)]
 
-        kv = kT.rearrange("h (p j) n -> (h p) j n", j=4)
-        qv = qT.rearrange("h (p j) n -> (h p) j n", j=4)
+        t_raw, t_abs, t_root, t_sign, kb_raw, kb_half = [
+            tile(name, [P, PACK], F32) for name in ("t_raw", "t_abs", "t_root", "t_sign", "kb_raw", "kb_half")]
 
-        def copy(eng, out, in_):
-            if eng == "V":
-                nc.vector.tensor_copy(out=out, in_=in_)
-            else:
-                nc.scalar.copy(out=out, in_=in_)
+        k_raw = [tile("k_raw%d" % m, [P, PACK, HALF], F32) for m in range(2)]
+        q_raw = [tile("q_raw%d" % g, [P, PACK, QB * n], F32) for g, (first, n) in enumerate(GROUPS)]
+        v_raw = [tile("v_raw%d" % h, [P, PACK, E], F32) for h in range(H)]
+        k_bf = tile("k_bf", [P, PACK, P, PACK], BF16)
+        q_bf = tile("q_bf", [P, NQ, PACK], BF16)
+        v_bf = tile("v_bf", [P, H, E, PACK], BF16)
+        w_bf = [tile("w_bf%d" % h, [P, NQ, PACK], BF16) for h in range(H)]
+        k_words, k_scales = tile("k_words", [P, PACK, P], U32), tile("k_scales", [P, PACK, P], U8)
+        q_words, q_scales = tile("q_words", [P, NQ], U32), tile("q_scales", [P, NQ], U8)
+        v_words, v_scales = tile("v_words", [P, H, E], U32), tile("v_scales", [P, H, E], U8)
+        w_words = [tile("w_words%d" % h, [P, NQ], U32) for h in range(H)]
+        w_scales = [tile("w_scales%d" % h, [P, NQ], U8) for h in range(H)]
+        capped = [tile("capped%d" % g, [P, PACK, H, QB * n], F32) for g, (first, n) in enumerate(GROUPS)]
+        u = [tile("u%d" % g, [P, PACK, H, QB * n], F32) for g, (first, n) in enumerate(GROUPS)]
+        denom, inverse, result = {}, {}, {}
 
-        def units(s):
-            return [(int(s[i]), int(s[i + 1])) for i in range(0, len(s), 2)]
+        def blocks(first, n):
+            return slice(QB * first, QB * (first + n))
 
-        def yview(us):
-            b, s = YSLOT[us[0]]
-            return banks[b][:, 128 * s : 128 * (s + len(us))].rearrange("p (n e) -> p n e", e=E)
+        def group_of(block):
+            return max(g for g, (first, n) in enumerate(GROUPS) if first <= block)
+
+        def load_queries(g):
+            nc.sync.dma_start(out=q_raw[g][:], in_=qT.rearrange("h (p j) q -> (h p) j q", j=PACK)[:, :, blocks(*GROUPS[g])])
+
+        def load_values(h):
+            nc.sync.dma_start(out=v_raw[h][:], in_=v[h].rearrange("(p r) e -> p r e", r=PACK))
+
+        def round_keys(m):
+            for quarter in range(2):
+                tokens = slice(128 * quarter, 128 * (quarter + 1))
+                s0 = (HALF * m + 128 * quarter) // PACK
+                nc.vector.tensor_copy(out=k_bf[:, :, s0 : s0 + 128 // PACK, :].rearrange("p r s j -> p s j r"),
+                                      in_=k_raw[m][:, :, tokens].rearrange("p j (s r) -> p s j r", r=PACK))
+
+        def quantise_keys(r, m):
+            cols = slice(64 * m, 64 * (m + 1))
+            nc.vector.quantize_mx(out=k_words[:, r, cols].bitcast(FP8X4), scales=k_scales[:, r, cols],
+                                  in_=k_bf[:, r, cols, :].rearrange("p s j -> p (s j)"))
+
+        def round_queries(block):
+            g = group_of(block)
+            nc.vector.tensor_copy(
+                out=q_bf[:, blocks(block, 1), :].rearrange("p (c i) j -> p c j i", i=RUN),
+                in_=q_raw[g][:, :, blocks(block - GROUPS[g][0], 1)].rearrange("p j (c i) -> p c j i", i=RUN))
+
+        def quantise_queries(g):
+            cols = blocks(*GROUPS[g])
+            nc.vector.quantize_mx(out=q_words[:, cols].bitcast(FP8X4), scales=q_scales[:, cols],
+                                  in_=q_bf[:, cols, :].rearrange("p q j -> p (q j)"))
+
+        def round_values(h):
+            nc.vector.tensor_tensor(out=v_bf[:, h, :, :].rearrange("p (c i) r -> p c r i", i=RUN),
+                                    in0=v_raw[h][:].rearrange("p r (c i) -> p c r i", i=RUN),
+                                    in1=t_sign[:].unsqueeze(1).unsqueeze(3).to_broadcast([P, E // RUN, PACK, RUN]),
+                                    op=ALU.mult)
+
+        def quantise_values(h):
+            nc.vector.quantize_mx(out=v_words[:, h, :].bitcast(FP8X4), scales=v_scales[:, h, :],
+                                  in_=v_bf[:, h, :, :].rearrange("p e r -> p (e r)"))
+
+        def scores(step):
+            g, r = STEPS[step]
+            first, n = GROUPS[g]
+            for i in range(n):
+                cols = blocks(first + i, 1)
+                for h in range(H):
+                    rows = slice(ROWS * h, ROWS * (h + 1))
+                    nc.tensor.matmul_mx(out=score_bank[h][step % SCORE_BANKS][:, blocks(i, 1)],
+                                        lhsT=k_words[rows, r, :].bitcast(FP8X4), lhsT_scale=k_scales[rows, r, :],
+                                        rhs=q_words[rows, cols].bitcast(FP8X4), rhs_scale=q_scales[rows, cols],
+                                        start=True, stop=True)
+
+        def cap(step):
+            g, r = STEPS[step]
+            for h in range(H):
+                nc.scalar.activation(out=capped[g][:, r, h, :], in_=score_bank[h][step % SCORE_BANKS][:, blocks(0, GROUPS[g][1])],
+                                     func=ACT.Tanh, bias=kb_half[:, r : r + 1], scale=0.5)
+
+        def cap_and_refill(g):
+            for step in range(PACK * g, PACK * (g + 1)):
+                cap(step)
+                if step + SCORE_BANKS < len(STEPS):
+                    scores(step + SCORE_BANKS)
+
+        def relu_scale(g, r, heads=slice(0, H)):
+            nc.vector.tensor_scalar(out=u[g][:, r, heads, :], in0=capped[g][:, r, heads, :], scalar1=0.0,
+                                    scalar2=t_root[:, r : r + 1], op0=ALU.max, op1=ALU.mult)
+
+        def square_views(block, h):
+            g = group_of(block)
+            src = u[g][:, :, h, blocks(block - GROUPS[g][0], 1)].rearrange("p r (c i) -> p c r i", i=RUN)
+            dst = w_bf[h][:, blocks(block, 1), :].rearrange("p (c i) r -> p c r i", i=RUN)
+            return dst, src
+
+        def square_on_vector(block, h):
+            dst, src = square_views(block, h)
+            nc.vector.tensor_tensor(out=dst, in0=src, in1=src, op=ALU.mult)
+
+        def square_on_scalar(block, h):
+            dst, src = square_views(block, h)
+            nc.scalar.activation(out=dst, in_=src, func=ACT.Square)
+
+        def quantise_weights(block, h, n=1):
+            cols = blocks(block, n)
+            nc.vector.quantize_mx(out=w_words[h][:, cols].bitcast(FP8X4), scales=w_scales[h][:, cols],
+                                  in_=w_bf[h][:, cols, :].rearrange("p q r -> p (q r)"))
+
+        def second_product(block, h, n=1):
+            for b in range(block, block + n):
+                bank, place = Y_PLACE[(b, h)]
+                nc.tensor.matmul_mx(out=y_bank[bank][:, place, :],
+                                    lhsT=w_words[h][:, blocks(b, 1)].bitcast(FP8X4), lhsT_scale=w_scales[h][:, blocks(b, 1)],
+                                    rhs=v_words[:, h, :].bitcast(FP8X4), rhs_scale=v_scales[:, h, :],
+                                    start=True, stop=True)
+
+        def y_view(block, h, n):
+            bank, place = Y_PLACE[(block, h)]
+            return y_bank[bank][:, place : place + n, :]
+
+        def denominator_on_vector(block, h, n=1):
+            denom[(block, h)] = tile("denom%d%d" % (block, h), [P, n], F32)
+            nc.vector.tensor_scalar_add(out=denom[(block, h)][:], in0=y_view(block, h, n)[:, :, E - 1], scalar1=1.0)
+
+        def denominator_on_scalar(block, h):
+            denom[(block, h)] = tile("denom%d%d" % (block, h), [P, 1], F32)
+            nc.scalar.activation(out=denom[(block, h)][:], in_=y_view(block, h, 1)[:, :, E - 1], func=ACT.Copy, bias=1.0)
+
+        def invert(block, h, n=1):
+            inverse[(block, h)] = tile("inverse%d%d" % (block, h), [P, n], F32)
+            nc.vector.reciprocal(out=inverse[(block, h)][:], in_=denom[(block, h)][:])
+
+        def divide_on_vector(block, h, n=1):
+            result[(block, h)] = tile("result%d%d" % (block, h), [P, n, E], F32)
+            nc.vector.tensor_tensor(out=result[(block, h)][:], in0=y_view(block, h, n),
+                                    in1=inverse[(block, h)][:].unsqueeze(2).to_broadcast([P, n, E]), op=ALU.mult)
+
+        def divide_on_scalar(block, h, n=1):
+            result[(block, h)] = tile("result%d%d" % (block, h), [P, n, E], F32)
+            for i in range(n):
+                nc.scalar.activation(out=result[(block, h)][:, i, :], in_=y_view(block, h, n)[:, i, :], func=ACT.Copy,
+                                     scale=inverse[(block, h)][:, i : i + 1])
+
+        def store(block, h, n=1):
+            nc.sync.dma_start(out=out[h, blocks(block, n), :].rearrange("(b p) e -> p b e", p=P), in_=result[(block, h)][:])
 
         ctx.enter_context(tc.manual_schedule())
-        nc.scalar.dma_start(out=t_raw[:], in_=t.rearrange("(p r) o -> p (r o)", r=4))
-        nc.sync.dma_start(out=k_raw[0][:], in_=kv[:, :, 0:256])
-        nc.sync.dma_start(out=k_raw[1][:], in_=kv[:, :, 256:512])
-        nc.sync.dma_start(out=q_raw[0][:], in_=qv[:, :, 0:256])
-        nc.sync.dma_start(out=kb_raw[:], in_=kb.rearrange("(p r) o -> p (r o)", r=4))
-        nc.sync.dma_start(out=q_raw[1][:], in_=qv[:, :, 256:512])
-        for h in range(H):
-            nc.sync.dma_start(out=v_raw[h][:], in_=v[h].rearrange("(p j) e -> p j e", j=4))
-        if USEPOW:
-            nc.gpsimd.memset(half[:], 0.5)
 
-        for name, eng in ORDER:
-            if name == "abs":
-                nc.vector.scalar_tensor_tensor(out=t_abs[:], in0=t_raw[:], scalar=-1.0, in1=t_raw[:], op0=ALU.mult, op1=ALU.max)
-            elif name == "pow":
-                nc.gpsimd.tensor_tensor(out=t_pow[:], in0=t_abs[:], in1=half[:], op=ALU.pow)
-            elif name == "root":
-                if USEPOW:
-                    nc.scalar.activation(out=root[:], in_=t_pow[:], func=ACT.Copy, scale=2.0)
-                else:
-                    nc.scalar.activation(out=root[:], in_=t_abs[:], func=ACT.Sqrt, scale=4.0)
-            elif name == "sign":
-                nc.scalar.activation(out=sign[:], in_=t_raw[:], func=ACT.Sign)
-            elif name == "prepk":
-                nc.vector.tensor_scalar_mul(out=kb_half[:], in0=kb_raw[:], scalar1=0.5)
-            elif name.startswith("ck"):
-                m, i = int(name[2]), int(name[3])
-                s0 = 64 * m + 32 * i
-                copy(eng, k_bf[:, :, s0 : s0 + 32, :].rearrange("p r s j -> p s j r"),
-                     k_raw[m][:, :, 128 * i : 128 * i + 128].rearrange("p j (s r) -> p s j r", r=4))
-            elif name.startswith("qk"):
-                r, m = int(name[2]), int(name[3])
-                nc.vector.quantize_mx(out=k_c[:, r, 64 * m : 64 * m + 64].bitcast(FP8X4), scales=k_s[:, r, 64 * m : 64 * m + 64],
-                                      in_=k_bf[:, r, 64 * m : 64 * m + 64, :].rearrange("p s j -> p (s j)"))
-            elif name.startswith("cq"):
-                c = int(name[2])
-                copy(eng, q_bf[:, 128 * c : 128 * c + 128, :].rearrange("p (n i) j -> p n j i", i=RUN),
-                     q_raw[c // 2][:, :, 128 * (c % 2) : 128 * (c % 2) + 128].rearrange("p j (n i) -> p n j i", i=RUN))
-            elif name.startswith("qq"):
-                c = int(name[2])
-                cols = slice(128 * c, 128 * (c + QQ[c]))
-                nc.vector.quantize_mx(out=q_c[:, cols].bitcast(FP8X4), scales=q_s[:, cols], in_=q_bf[:, cols, :].rearrange("p n j -> p (n j)"))
-            elif name.startswith("cv"):
-                h = int(name[2])
-                nc.vector.tensor_tensor(out=v_bf[:, h, :, :].rearrange("p (n i) j -> p n j i", i=RUN),
-                                        in0=v_raw[h][:].rearrange("p j (n i) -> p n j i", i=RUN),
-                                        in1=sign[:].unsqueeze(1).unsqueeze(3).to_broadcast([P, E // RUN, 4, RUN]), op=ALU.mult)
-            elif name.startswith("qv"):
-                h = int(name[2])
-                nc.vector.quantize_mx(out=v_c[:, h, :].bitcast(FP8X4), scales=v_s[:, h, :], in_=v_bf[:, h, :, :].rearrange("p e j -> p (e j)"))
-            elif name.startswith("mm"):
-                c, h, r = int(name[2]), int(name[3]), int(name[4])
-                b, s = SBANK[(2 * (c // 2), h, r)]
-                s += c % 2
-                rows = slice(64 * h, 64 * h + 64)
-                cols = slice(128 * c, 128 * c + 128)
-                nc.tensor.matmul_mx(out=banks[b][:, 128 * s : 128 * s + 128], lhsT=k_c[rows, r, :].bitcast(FP8X4), lhsT_scale=k_s[rows, r, :],
-                                    rhs=q_c[rows, cols].bitcast(FP8X4), rhs_scale=q_s[rows, cols], start=True, stop=True)
-            elif name[0] == "T":
-                c, h, r = int(name[1]), int(name[2]), int(name[3])
-                b, s = SBANK[(c, h, r)]
-                nc.scalar.activation(out=th[(c // 2, h)][:, r, :], in_=banks[b][:, 128 * s : 128 * s + 256], func=ACT.Tanh,
-                                     bias=kb_half[:, r : r + 1], scale=0.5)
-            elif name[0] == "A":
-                c, h, r = int(name[1]), int(name[2]), int(name[3])
-                nc.vector.tensor_scalar(out=u[(c // 2, h)][:, r, :], in0=th[(c // 2, h)][:, r, :], scalar1=0.0, scalar2=root[:, r : r + 1],
-                                        op0=ALU.max, op1=ALU.mult)
-            elif name[0] == "B":
-                c, h = int(name[1]), int(name[2])
-                src = u[(c // 2, h)][:, :, 128 * (c % 2) : 128 * (c % 2) + 128].rearrange("p r (n i) -> p n r i", i=RUN)
-                dst = w_bf[(c, h)][:].rearrange("p (n i) r -> p n r i", i=RUN)
-                if eng == "V":
-                    nc.vector.tensor_tensor(out=dst, in0=src, in1=src, op=ALU.mult)
-                else:
-                    nc.scalar.activation(out=dst, in_=src, func=ACT.Square)
-            elif name[0] == "Q":
-                c, h = int(name[1]), int(name[2])
-                nc.vector.quantize_mx(out=w_c[(c, h)][:].bitcast(FP8X4), scales=w_s[(c, h)][:], in_=w_bf[(c, h)][:].rearrange("p n r -> p (n r)"))
-            elif name[0] == "y":
-                c, h = int(name[1]), int(name[2])
-                b, s = YSLOT[(c, h)]
-                nc.tensor.matmul_mx(out=banks[b][:, 128 * s : 128 * s + 128], lhsT=w_c[(c, h)][:].bitcast(FP8X4), lhsT_scale=w_s[(c, h)][:],
-                                    rhs=v_c[:, h, :].bitcast(FP8X4), rhs_scale=v_s[:, h, :], start=True, stop=True)
-            elif name.startswith("den"):
-                key = name[3:]
-                us = units(key)
-                den[key] = tile([P, len(us)], F32, "den" + key)
-                src = yview(us)[:, :, E - 1]
-                if eng == "V":
-                    nc.vector.tensor_scalar_add(out=den[key][:], in0=src, scalar1=1.0)
-                else:
-                    nc.scalar.activation(out=den[key][:], in_=src, func=ACT.Copy, bias=1.0)
-            elif name.startswith("rc"):
-                key = name[2:]
-                rec[key] = tile([P, len(key) // 2], F32, "rec" + key)
-                nc.vector.reciprocal(out=rec[key][:], in_=den[key][:])
-            elif name[0] == "E":
-                key = name[1:]
-                us = units(key)
-                res[key] = tile([P, len(us), E], F32, "res" + key)
-                if eng == "V":
-                    nc.vector.tensor_tensor(out=res[key][:], in0=yview(us), in1=rec[key][:].unsqueeze(2).to_broadcast([P, len(us), E]), op=ALU.mult)
-                else:
-                    for i in range(len(us)):
-                        nc.scalar.activation(out=res[key][:, i, :], in_=yview(us)[:, i, :], func=ACT.Copy, scale=rec[key][:, i : i + 1])
-            elif name.startswith("st"):
-                key = name[2:]
-                us = units(key)
-                c, h = us[0]
-                nc.sync.dma_start(out=out[h, 128 * c : 128 * (c + len(us)), :].rearrange("(n p) e -> p n e", p=P), in_=res[key][:])
+        nc.sync.dma_start(out=t_raw[:], in_=t.rearrange("(s r) o -> s (r o)", r=PACK))
+        for m in range(2):
+            nc.sync.dma_start(out=k_raw[m][:],
+                              in_=kT.rearrange("h (p j) i -> (h p) j i", j=PACK)[:, :, HALF * m : HALF * (m + 1)])
+        load_queries(0)
+        nc.sync.dma_start(out=kb_raw[:], in_=kb.rearrange("(s r) o -> s (r o)", r=PACK))
+        load_queries(1)
+        load_values(0)
+        load_queries(2)
+        load_values(1)
+
+        nc.vector.scalar_tensor_tensor(out=t_abs[:], in0=t_raw[:], scalar=-1.0, in1=t_raw[:], op0=ALU.mult, op1=ALU.max)
+        nc.scalar.activation(out=t_root[:], in_=t_abs[:], func=ACT.Sqrt, scale=4.0)
+        nc.scalar.activation(out=t_sign[:], in_=t_raw[:], func=ACT.Sign)
+
+        round_keys(0)
+        for r in range(3):
+            quantise_keys(r, 0)
+        round_keys(1)
+        round_queries(0)
+        nc.vector.tensor_scalar_mul(out=kb_half[:], in0=kb_raw[:], scalar1=0.5)
+        quantise_keys(0, 1)
+        quantise_queries(0)
+        quantise_keys(1, 1)
+        round_queries(1)
+        quantise_keys(2, 1)
+        quantise_keys(3, 0)
+        quantise_keys(3, 1)
+        quantise_queries(1)
+        round_values(0)
+        for step in range(SCORE_BANKS):
+            scores(step)
+
+        cap_and_refill(0)
+        relu_scale(0, 0)
+        round_queries(2)
+        round_queries(3)
+        relu_scale(0, 1)
+        relu_scale(0, 2)
+        quantise_queries(2)
+        relu_scale(0, 3)
+        quantise_values(0)
+
+        cap_and_refill(1)
+        for r in range(PACK):
+            relu_scale(1, r)
+        round_values(1)
+        square_on_scalar(0, 0)
+        square_on_vector(1, 0)
+        square_on_vector(0, 1)
+        quantise_weights(0, 0, n=2)
+
+        cap_and_refill(2)
+        second_product(0, 0, n=2)
+        for r in range(PACK):
+            for h in range(H):
+                relu_scale(2, r, slice(h, h + 1))
+        quantise_values(1)
+
+        square_on_scalar(1, 1)
+        denominator_on_vector(0, 0, n=2)
+        quantise_weights(0, 1, n=2)
+        second_product(0, 1, n=2)
+        invert(0, 0, n=2)
+        square_on_scalar(2, 0)
+        square_on_vector(3, 0)
+        quantise_weights(2, 0)
+        second_product(2, 0)
+        denominator_on_vector(0, 1, n=2)
+        quantise_weights(3, 0)
+        second_product(3, 0)
+        invert(0, 1, n=2)
+        square_on_scalar(2, 1)
+        quantise_weights(2, 1)
+        second_product(2, 1)
+        divide_on_vector(0, 0, n=2)
+        store(0, 0, n=2)
+        denominator_on_vector(2, 0)
+        square_on_scalar(3, 1)
+        quantise_weights(3, 1)
+        second_product(3, 1)
+        invert(2, 0)
+        denominator_on_scalar(2, 1)
+        denominator_on_scalar(3, 0)
+        invert(2, 1)
+        invert(3, 0)
+        divide_on_scalar(0, 1, n=2)
+        store(0, 1, n=2)
+        denominator_on_vector(3, 1)
+        divide_on_scalar(2, 1)
+        store(2, 1)
+        divide_on_vector(2, 0)
+        store(2, 0)
+        divide_on_scalar(3, 0)
+        store(3, 0)
+        invert(3, 1)
+        divide_on_vector(3, 1)
+        store(3, 1)

@@ -190,12 +190,12 @@ def tile_rows_a_relu2_kb_cap_kernel(tc, qT, kT, t, v, kb, out):
 
         ctx.enter_context(tc.manual_schedule())
 
-        nc.sync.dma_start(out=t_raw[:], in_=t.rearrange("(s r) o -> s (r o)", r=PACK))
+        nc.scalar.dma_start(out=t_raw[:], in_=t.rearrange("(s r) o -> s (r o)", r=PACK))
+        nc.scalar.dma_start(out=kb_raw[:], in_=kb.rearrange("(s r) o -> s (r o)", r=PACK))
         for m in range(2):
             nc.sync.dma_start(out=k_raw[m][:],
                               in_=kT.rearrange("h (p j) i -> (h p) j i", j=PACK)[:, :, HALF * m : HALF * (m + 1)])
         load_queries(0)
-        nc.sync.dma_start(out=kb_raw[:], in_=kb.rearrange("(s r) o -> s (r o)", r=PACK))
         load_queries(1)
         load_values(0)
         load_queries(2)

@@ -23,6 +23,7 @@ RUN = 4
 GROUPS = [(0, 1), (1, 1), (2, 2)]
 STEPS = [(g, r) for g in range(len(GROUPS)) for r in range(PACK)]
 SCORE_BANKS = 3
+FILLS = [[0], [1], [2, 3], [4, 5], [6, 7], [8], [9], [10], [11]]
 Y_PLACE = {(0, 0): (0, 0), (1, 0): (0, 1), (2, 0): (0, 2), (3, 1): (0, 3),
            (0, 1): (1, 0), (1, 1): (1, 1), (3, 0): (1, 2), (2, 1): (1, 3)}
 
@@ -42,11 +43,11 @@ def tile_rows_a_relu2_kb_cap_kernel(tc, qT, kT, t, v, kb, out):
         t_raw, t_abs, t_root, t_sign, kb_raw, kb_half = [
             tile(name, [P, PACK], F32) for name in ("t_raw", "t_abs", "t_root", "t_sign", "kb_raw", "kb_half")]
 
-        k_raw = [tile("k_raw%d" % m, [P, PACK, HALF], F32) for m in range(2)]
+        k_raw = [tile("k_raw%d" % m, [P, PACK, P // 2, PACK], F32) for m in range(2)]
         q_raw = [tile("q_raw%d" % g, [P, PACK, QB * n], F32) for g, (first, n) in enumerate(GROUPS)]
         v_raw = [tile("v_raw%d" % h, [P, PACK, E], F32) for h in range(H)]
-        k_bf = tile("k_bf", [P, PACK, P, PACK], BF16)
-        q_bf = tile("q_bf", [P, NQ, PACK], BF16)
+        k_bf = [tile("k_bf%d" % m, [P, PACK, P // 2, PACK], BF16) for m in range(2)]
+        q_bf = [tile("q_bf%d" % g, [P, QB * n, PACK], BF16) for g, (first, n) in enumerate(GROUPS)]
         v_bf = tile("v_bf", [P, H, E, PACK], BF16)
         w_bf = [tile("w_bf%d" % h, [P, NQ, PACK], BF16) for h in range(H)]
         k_words, k_scales = tile("k_words", [P, PACK, P], U32), tile("k_scales", [P, PACK, P], U8)
@@ -70,28 +71,31 @@ def tile_rows_a_relu2_kb_cap_kernel(tc, qT, kT, t, v, kb, out):
         def load_values(h):
             nc.sync.dma_start(out=v_raw[h][:], in_=v[h].rearrange("(p r) e -> p r e", r=PACK))
 
-        def round_keys(m):
-            for quarter in range(2):
-                tokens = slice(128 * quarter, 128 * (quarter + 1))
-                s0 = (HALF * m + 128 * quarter) // PACK
-                nc.vector.tensor_copy(out=k_bf[:, :, s0 : s0 + 128 // PACK, :].rearrange("p r s j -> p s j r"),
-                                      in_=k_raw[m][:, :, tokens].rearrange("p j (s r) -> p s j r", r=PACK))
+        def load_keys(m):
+            nc.sync.dma_start(out=k_raw[m][:].rearrange("p j s r -> p j (s r)"),
+                              in_=kT.rearrange("h (p j) i -> (h p) j i", j=PACK)[:, :, HALF * m : HALF * (m + 1)])
+
+        def key_views(m, tiles=slice(0, PACK)):
+            return k_bf[m][:, tiles, :, :].rearrange("p r s j -> p s j r"), k_raw[m][:, :, :, tiles].rearrange("p j s r -> p s j r")
 
         def quantise_keys(r, m):
             cols = slice(64 * m, 64 * (m + 1))
             nc.vector.quantize_mx(out=k_words[:, r, cols].bitcast(FP8X4), scales=k_scales[:, r, cols],
-                                  in_=k_bf[:, r, cols, :].rearrange("p s j -> p (s j)"))
+                                  in_=k_bf[m][:, r, :, :].rearrange("p s j -> p (s j)"))
 
-        def round_queries(block):
-            g = group_of(block)
-            nc.vector.tensor_copy(
-                out=q_bf[:, blocks(block, 1), :].rearrange("p (c i) j -> p c j i", i=RUN),
-                in_=q_raw[g][:, :, blocks(block - GROUPS[g][0], 1)].rearrange("p j (c i) -> p c j i", i=RUN))
+        def query_views(g):
+            return (q_bf[g][:].rearrange("p (c i) j -> p c j i", i=RUN), q_raw[g][:].rearrange("p j (c i) -> p c j i", i=RUN))
+
+        def round_on_vector(views):
+            nc.vector.tensor_copy(out=views[0], in_=views[1])
+
+        def round_on_scalar(views):
+            nc.scalar.copy(out=views[0], in_=views[1])
 
         def quantise_queries(g):
             cols = blocks(*GROUPS[g])
             nc.vector.quantize_mx(out=q_words[:, cols].bitcast(FP8X4), scales=q_scales[:, cols],
-                                  in_=q_bf[:, cols, :].rearrange("p q j -> p (q j)"))
+                                  in_=q_bf[g][:].rearrange("p q j -> p (q j)"))
 
         def round_values(h):
             nc.vector.tensor_tensor(out=v_bf[:, h, :, :].rearrange("p (c i) r -> p c r i", i=RUN),
@@ -103,46 +107,46 @@ def tile_rows_a_relu2_kb_cap_kernel(tc, qT, kT, t, v, kb, out):
             nc.vector.quantize_mx(out=v_words[:, h, :].bitcast(FP8X4), scales=v_scales[:, h, :],
                                   in_=v_bf[:, h, :, :].rearrange("p e r -> p (e r)"))
 
-        def scores(step):
-            g, r = STEPS[step]
-            first, n = GROUPS[g]
-            for i in range(n):
-                cols = blocks(first + i, 1)
-                for h in range(H):
-                    rows = slice(ROWS * h, ROWS * (h + 1))
-                    nc.tensor.matmul_mx(out=score_bank[h][step % SCORE_BANKS][:, blocks(i, 1)],
-                                        lhsT=k_words[rows, r, :].bitcast(FP8X4), lhsT_scale=k_scales[rows, r, :],
-                                        rhs=q_words[rows, cols].bitcast(FP8X4), rhs_scale=q_scales[rows, cols],
-                                        start=True, stop=True)
+        def score_view(step, h, first, n):
+            fill = [step in steps for steps in FILLS].index(True)
+            return score_bank[h][fill % SCORE_BANKS][:, blocks(FILLS[fill].index(step) + first, n)]
 
-        def cap(step):
-            g, r = STEPS[step]
+        def scores(fill):
             for h in range(H):
-                nc.scalar.activation(out=capped[g][:, r, h, :], in_=score_bank[h][step % SCORE_BANKS][:, blocks(0, GROUPS[g][1])],
-                                     func=ACT.Tanh, bias=kb_half[:, r : r + 1], scale=0.5)
+                for step in FILLS[fill]:
+                    g, r = STEPS[step]
+                    first, n = GROUPS[g]
+                    for i in range(n):
+                        cols = blocks(first + i, 1)
+                        rows = slice(ROWS * h, ROWS * (h + 1))
+                        nc.tensor.matmul_mx(out=score_view(step, h, i, 1),
+                                            lhsT=k_words[rows, r, :].bitcast(FP8X4), lhsT_scale=k_scales[rows, r, :],
+                                            rhs=q_words[rows, cols].bitcast(FP8X4), rhs_scale=q_scales[rows, cols],
+                                            start=True, stop=True)
 
-        def cap_and_refill(g):
-            for step in range(PACK * g, PACK * (g + 1)):
-                cap(step)
-                if step + SCORE_BANKS < len(STEPS):
-                    scores(step + SCORE_BANKS)
+        def cap(step, heads=range(H)):
+            g, r = STEPS[step]
+            for h in heads:
+                nc.scalar.activation(out=capped[g][:, r, h, :], in_=score_view(step, h, 0, GROUPS[g][1]),
+                                     func=ACT.Tanh, bias=kb_half[:, r : r + 1], scale=0.5)
 
         def relu_scale(g, r, heads=slice(0, H)):
             nc.vector.tensor_scalar(out=u[g][:, r, heads, :], in0=capped[g][:, r, heads, :], scalar1=0.0,
                                     scalar2=t_root[:, r : r + 1], op0=ALU.max, op1=ALU.mult)
 
-        def square_views(block, h):
+        def square_views(block, h, part):
             g = group_of(block)
-            src = u[g][:, :, h, blocks(block - GROUPS[g][0], 1)].rearrange("p r (c i) -> p c r i", i=RUN)
-            dst = w_bf[h][:, blocks(block, 1), :].rearrange("p (c i) r -> p c r i", i=RUN)
+            first = QB * (block - GROUPS[g][0])
+            src = u[g][:, :, h, first + part.start : first + part.stop].rearrange("p r (c i) -> p c r i", i=RUN)
+            dst = w_bf[h][:, QB * block + part.start : QB * block + part.stop, :].rearrange("p (c i) r -> p c r i", i=RUN)
             return dst, src
 
-        def square_on_vector(block, h):
-            dst, src = square_views(block, h)
+        def square_on_vector(block, h, part=range(QB)):
+            dst, src = square_views(block, h, part)
             nc.vector.tensor_tensor(out=dst, in0=src, in1=src, op=ALU.mult)
 
-        def square_on_scalar(block, h):
-            dst, src = square_views(block, h)
+        def square_on_scalar(block, h, part=range(QB)):
+            dst, src = square_views(block, h, part)
             nc.scalar.activation(out=dst, in_=src, func=ACT.Square)
 
         def quantise_weights(block, h, n=1):
@@ -166,18 +170,21 @@ def tile_rows_a_relu2_kb_cap_kernel(tc, qT, kT, t, v, kb, out):
             denom[(block, h)] = tile("denom%d%d" % (block, h), [P, n], F32)
             nc.vector.tensor_scalar_add(out=denom[(block, h)][:], in0=y_view(block, h, n)[:, :, E - 1], scalar1=1.0)
 
-        def denominator_on_scalar(block, h):
-            denom[(block, h)] = tile("denom%d%d" % (block, h), [P, 1], F32)
-            nc.scalar.activation(out=denom[(block, h)][:], in_=y_view(block, h, 1)[:, :, E - 1], func=ACT.Copy, bias=1.0)
+        def denominator_on_scalar(block, h, n=1):
+            denom[(block, h)] = tile("denom%d%d" % (block, h), [P, n], F32)
+            nc.scalar.activation(out=denom[(block, h)][:], in_=y_view(block, h, n)[:, :, E - 1], func=ACT.Copy, bias=1.0)
 
         def invert(block, h, n=1):
             inverse[(block, h)] = tile("inverse%d%d" % (block, h), [P, n], F32)
             nc.vector.reciprocal(out=inverse[(block, h)][:], in_=denom[(block, h)][:])
 
+        def share_inverse(owner, block, h, first, n):
+            inverse[(block, h)] = inverse[owner][:, first : first + n]
+
         def divide_on_vector(block, h, n=1):
             result[(block, h)] = tile("result%d%d" % (block, h), [P, n, E], F32)
             nc.vector.tensor_tensor(out=result[(block, h)][:], in0=y_view(block, h, n),
-                                    in1=inverse[(block, h)][:].unsqueeze(2).to_broadcast([P, n, E]), op=ALU.mult)
+                                    in1=inverse[(block, h)][:, 0:n].unsqueeze(2).to_broadcast([P, n, E]), op=ALU.mult)
 
         def divide_on_scalar(block, h, n=1):
             result[(block, h)] = tile("result%d%d" % (block, h), [P, n, E], F32)
@@ -192,9 +199,8 @@ def tile_rows_a_relu2_kb_cap_kernel(tc, qT, kT, t, v, kb, out):
 
         nc.scalar.dma_start(out=t_raw[:], in_=t.rearrange("(s r) o -> s (r o)", r=PACK))
         nc.scalar.dma_start(out=kb_raw[:], in_=kb.rearrange("(s r) o -> s (r o)", r=PACK))
-        for m in range(2):
-            nc.sync.dma_start(out=k_raw[m][:],
-                              in_=kT.rearrange("h (p j) i -> (h p) j i", j=PACK)[:, :, HALF * m : HALF * (m + 1)])
+        load_keys(0)
+        load_keys(1)
         load_queries(0)
         load_queries(1)
         load_values(0)
@@ -205,35 +211,50 @@ def tile_rows_a_relu2_kb_cap_kernel(tc, qT, kT, t, v, kb, out):
         nc.scalar.activation(out=t_root[:], in_=t_abs[:], func=ACT.Sqrt, scale=4.0)
         nc.scalar.activation(out=t_sign[:], in_=t_raw[:], func=ACT.Sign)
 
-        round_keys(0)
-        for r in range(3):
+        round_on_vector(key_views(0))
+        for r in range(PACK):
             quantise_keys(r, 0)
-        round_keys(1)
-        round_queries(0)
+        round_on_vector(key_views(1))
+        round_on_vector(query_views(0))
         nc.vector.tensor_scalar_mul(out=kb_half[:], in0=kb_raw[:], scalar1=0.5)
         quantise_keys(0, 1)
         quantise_queries(0)
         quantise_keys(1, 1)
-        round_queries(1)
+        round_on_vector(query_views(1))
         quantise_keys(2, 1)
-        quantise_keys(3, 0)
         quantise_keys(3, 1)
         quantise_queries(1)
         round_values(0)
         for step in range(SCORE_BANKS):
             scores(step)
 
-        cap_and_refill(0)
+        cap(0)
+        scores(3)
+        cap(1)
+        scores(4)
+        cap(2, [0])
+        cap(3, [0])
+        cap(2, [1])
+        cap(3, [1])
         relu_scale(0, 0)
-        round_queries(2)
-        round_queries(3)
+        round_on_vector(query_views(2))
         relu_scale(0, 1)
         relu_scale(0, 2)
         quantise_queries(2)
+        scores(5)
         relu_scale(0, 3)
         quantise_values(0)
 
-        cap_and_refill(1)
+        cap(4, [0])
+        cap(5, [0])
+        cap(4, [1])
+        cap(5, [1])
+        scores(6)
+        cap(6, [0])
+        cap(7, [0])
+        cap(6, [1])
+        cap(7, [1])
+        scores(7)
         for r in range(PACK):
             relu_scale(1, r)
         round_values(1)
@@ -242,13 +263,17 @@ def tile_rows_a_relu2_kb_cap_kernel(tc, qT, kT, t, v, kb, out):
         square_on_vector(0, 1)
         quantise_weights(0, 0, n=2)
 
-        cap_and_refill(2)
+        cap(8)
+        scores(8)
+        cap(9)
+        cap(10)
+        cap(11)
         second_product(0, 0, n=2)
-        for r in range(PACK):
-            for h in range(H):
-                relu_scale(2, r, slice(h, h + 1))
+        for r in range(PACK - 1):
+            relu_scale(2, r)
+        for h in range(H):
+            relu_scale(2, PACK - 1, slice(h, h + 1))
         quantise_values(1)
-
         square_on_scalar(1, 1)
         denominator_on_vector(0, 0, n=2)
         quantise_weights(0, 1, n=2)

@@ -198,10 +198,10 @@ def tile_rows_a_relu2_kb_cap_kernel(tc, qT, kT, t, v, kb, out):
         ctx.enter_context(tc.manual_schedule())
 
         nc.scalar.dma_start(out=t_raw[:], in_=t.rearrange("(s r) o -> s (r o)", r=PACK))
-        nc.scalar.dma_start(out=kb_raw[:], in_=kb.rearrange("(s r) o -> s (r o)", r=PACK))
         load_keys(0)
-        load_keys(1)
         load_queries(0)
+        load_keys(1)
+        nc.sync.dma_start(out=kb_raw[:], in_=kb.rearrange("(s r) o -> s (r o)", r=PACK))
         load_queries(1)
         load_values(0)
         load_queries(2)
@@ -212,13 +212,14 @@ def tile_rows_a_relu2_kb_cap_kernel(tc, qT, kT, t, v, kb, out):
         nc.scalar.activation(out=t_sign[:], in_=t_raw[:], func=ACT.Sign)
 
         round_on_vector(key_views(0))
+        round_on_vector(query_views(0))
         for r in range(PACK):
             quantise_keys(r, 0)
-        round_on_vector(key_views(1))
-        round_on_vector(query_views(0))
+        quantise_queries(0)
+        round_on_vector(key_views(1, slice(0, 2)))
+        round_on_vector(key_views(1, slice(2, 4)))
         nc.vector.tensor_scalar_mul(out=kb_half[:], in0=kb_raw[:], scalar1=0.5)
         quantise_keys(0, 1)
-        quantise_queries(0)
         quantise_keys(1, 1)
         round_on_vector(query_views(1))
         quantise_keys(2, 1)

@@ -24,8 +24,8 @@ GROUPS = [(0, 1), (1, 1), (2, 2)]
 STEPS = [(g, r) for g in range(len(GROUPS)) for r in range(PACK)]
 SCORE_BANKS = 3
 FILLS = [[0], [1], [2, 3], [4, 5], [6, 7], [8], [9], [10], [11]]
-Y_PLACE = {(0, 0): (0, 0), (1, 0): (0, 1), (2, 0): (0, 2), (3, 1): (0, 3),
-           (0, 1): (1, 0), (1, 1): (1, 1), (3, 0): (1, 2), (2, 1): (1, 3)}
+Y_PLACE = {(0, 0): (0, 0), (1, 0): (0, 1), (2, 1): (0, 2), (3, 1): (0, 3),
+           (0, 1): (1, 0), (1, 1): (1, 1), (2, 0): (1, 2), (3, 0): (1, 3)}
 
 
 def tile_rows_a_relu2_kb_cap_kernel(tc, qT, kT, t, v, kb, out):
@@ -283,34 +283,29 @@ def tile_rows_a_relu2_kb_cap_kernel(tc, qT, kT, t, v, kb, out):
         square_on_scalar(2, 0)
         square_on_vector(3, 0)
         quantise_weights(2, 0)
-        second_product(2, 0)
         denominator_on_vector(0, 1, n=2)
+        second_product(2, 0)
         quantise_weights(3, 0)
         second_product(3, 0)
         invert(0, 1, n=2)
         square_on_scalar(2, 1)
         quantise_weights(2, 1)
-        second_product(2, 1)
-        divide_on_vector(0, 0, n=2)
-        store(0, 0, n=2)
-        denominator_on_vector(2, 0)
         square_on_scalar(3, 1)
+        divide_on_scalar(0, 0, n=2)
+        store(0, 0, n=2)
+        second_product(2, 1)
         quantise_weights(3, 1)
         second_product(3, 1)
-        invert(2, 0)
-        denominator_on_scalar(2, 1)
-        denominator_on_scalar(3, 0)
-        invert(2, 1)
-        invert(3, 0)
+        denominator_on_scalar(2, 0, n=2)
         divide_on_scalar(0, 1, n=2)
         store(0, 1, n=2)
-        denominator_on_vector(3, 1)
-        divide_on_scalar(2, 1)
+        invert(2, 0, n=2)
+        denominator_on_vector(2, 1, n=2)
+        divide_on_scalar(2, 0, n=2)
+        store(2, 0, n=2)
+        invert(2, 1, n=2)
+        share_inverse((2, 1), 3, 1, 1, 1)
+        divide_on_vector(2, 1)
         store(2, 1)
-        divide_on_vector(2, 0)
-        store(2, 0)
-        divide_on_scalar(3, 0)
-        store(3, 0)
-        invert(3, 1)
         divide_on_vector(3, 1)
         store(3, 1)

@@ -283,6 +283,7 @@ def tile_rows_a_relu2_kb_cap_kernel(tc, qT, kT, t, v, kb, out):
         square_on_scalar(2, 0)
         square_on_vector(3, 0)
         quantise_weights(2, 0)
+        square_on_vector(3, 1, range(64, QB))
         denominator_on_vector(0, 1, n=2)
         second_product(2, 0)
         quantise_weights(3, 0)
@@ -290,7 +291,7 @@ def tile_rows_a_relu2_kb_cap_kernel(tc, qT, kT, t, v, kb, out):
         invert(0, 1, n=2)
         square_on_scalar(2, 1)
         quantise_weights(2, 1)
-        square_on_scalar(3, 1)
+        square_on_scalar(3, 1, range(0, 64))
         divide_on_scalar(0, 0, n=2)
         store(0, 0, n=2)
         second_product(2, 1)

@@ -57,6 +57,7 @@ def tile_rows_a_relu2_kb_cap_kernel(tc, qT, kT, t, v, kb, out):
         w_scales = [tile("w_scales%d" % h, [P, NQ], U8) for h in range(H)]
         capped = [tile("capped%d" % g, [P, PACK, H, QB * n], F32) for g, (first, n) in enumerate(GROUPS)]
         u = [tile("u%d" % g, [P, PACK, H, QB * n], F32) for g, (first, n) in enumerate(GROUPS)]
+        warm = tile("warm", [P, 1], F32)
         denom, inverse, result = {}, {}, {}
 
         def blocks(first, n):
@@ -210,6 +211,7 @@ def tile_rows_a_relu2_kb_cap_kernel(tc, qT, kT, t, v, kb, out):
         nc.vector.scalar_tensor_tensor(out=t_abs[:], in0=t_raw[:], scalar=-1.0, in1=t_raw[:], op0=ALU.mult, op1=ALU.max)
         nc.scalar.activation(out=t_root[:], in_=t_abs[:], func=ACT.Sqrt, scale=4.0)
         nc.scalar.activation(out=t_sign[:], in_=t_raw[:], func=ACT.Sign)
+        nc.scalar.activation(out=warm[:], in_=t_raw[:, 0:1], func=ACT.Tanh)
 
         round_on_vector(key_views(0))
         round_on_vector(query_views(0))
@@ -217,7 +219,7 @@ def tile_rows_a_relu2_kb_cap_kernel(tc, qT, kT, t, v, kb, out):
             quantise_keys(r, 0)
         quantise_queries(0)
         round_on_vector(key_views(1, slice(0, 2)))
-        round_on_vector(key_views(1, slice(2, 4)))
+        round_on_scalar(key_views(1, slice(2, 4)))
         nc.vector.tensor_scalar_mul(out=kb_half[:], in0=kb_raw[:], scalar1=0.5)
         quantise_keys(0, 1)
         quantise_keys(1, 1)

@@ -21,11 +21,16 @@ HALF = N // 2
 RUN = 4
 
 GROUPS = [(0, 1), (1, 1), (2, 2)]
-STEPS = [(g, r) for g in range(len(GROUPS)) for r in range(PACK)]
-SCORE_BANKS = 3
-FILLS = [[0], [1], [2, 3], [4, 5], [6, 7], [8], [9], [10], [11]]
-Y_PLACE = {(0, 0): (0, 0), (1, 0): (0, 1), (2, 1): (0, 2), (3, 1): (0, 3),
-           (0, 1): (1, 0), (1, 1): (1, 1), (2, 0): (1, 2), (3, 0): (1, 3)}
+FILLS = [[(0, [0]), (0, [1]), (0, [2, 3]), (1, [0, 1]), (1, [2, 3]), (2, [0]), (2, [1]), (2, [2]), (2, [3])],
+         [(0, [0, 1]), (0, [2, 3]), (1, [0, 1]), (1, [2, 3]), (2, [0, 1]), (2, [2, 3])]]
+SCORE_BANKS = [3, 2]
+Y_BANKS = [[(0, 0), (1, 0), (0, 1), (1, 1)], [(2, 0), (3, 0)], [(2, 1), (3, 1)]]
+W_CALLS = [[(0, 0), (1, 0)], [(0, 1), (1, 1)], [(2, 0)], [(3, 0)], [(2, 1)], [(3, 1)]]
+
+
+def place_of(rows, unit):
+    row = [unit in units for units in rows].index(True)
+    return row, rows[row].index(unit)
 
 
 def tile_rows_a_relu2_kb_cap_kernel(tc, qT, kT, t, v, kb, out):
@@ -37,27 +42,27 @@ def tile_rows_a_relu2_kb_cap_kernel(tc, qT, kT, t, v, kb, out):
         def tile(name, shape, dtype):
             return sbuf.tile(shape, dtype, name=name, align_bytes=64)
 
-        score_bank = [[psum.tile([P, 512], F32, name="score%d%d" % (h, b)) for b in range(SCORE_BANKS)] for h in range(H)]
-        y_bank = [psum.tile([P, 4, E], F32, name="y%d" % b) for b in range(2)]
+        score_bank = [[psum.tile([P, 512], F32, name="score%d%d" % (h, b)) for b in range(SCORE_BANKS[h])] for h in range(H)]
+        y_bank = [psum.tile([P, 4, E], F32, name="y%d" % b) for b in range(len(Y_BANKS))]
 
         t_raw, t_abs, t_root, t_sign, kb_raw, kb_half = [
             tile(name, [P, PACK], F32) for name in ("t_raw", "t_abs", "t_root", "t_sign", "kb_raw", "kb_half")]
 
         k_raw = [tile("k_raw%d" % m, [P, PACK, P // 2, PACK], F32) for m in range(2)]
-        q_raw = [tile("q_raw%d" % g, [P, PACK, QB * n], F32) for g, (first, n) in enumerate(GROUPS)]
+        q_raw = [tile("q_raw%d" % b, [P, PACK, QB], F32) for b in range(NQ // QB)]
         v_raw = [tile("v_raw%d" % h, [P, PACK, E], F32) for h in range(H)]
         k_bf = [tile("k_bf%d" % m, [P, PACK, P // 2, PACK], BF16) for m in range(2)]
-        q_bf = [tile("q_bf%d" % g, [P, QB * n, PACK], BF16) for g, (first, n) in enumerate(GROUPS)]
+        warm = tile("warm", [P, 1], F32)
+        q_bf = [tile("q_bf%d" % b, [P, QB, PACK], BF16) for b in range(NQ // QB)]
         v_bf = tile("v_bf", [P, H, E, PACK], BF16)
-        w_bf = [tile("w_bf%d" % h, [P, NQ, PACK], BF16) for h in range(H)]
+        w_bf = [tile("w_bf%d" % c, [P, QB * len(units), PACK], BF16) for c, units in enumerate(W_CALLS)]
         k_words, k_scales = tile("k_words", [P, PACK, P], U32), tile("k_scales", [P, PACK, P], U8)
         q_words, q_scales = tile("q_words", [P, NQ], U32), tile("q_scales", [P, NQ], U8)
         v_words, v_scales = tile("v_words", [P, H, E], U32), tile("v_scales", [P, H, E], U8)
-        w_words = [tile("w_words%d" % h, [P, NQ], U32) for h in range(H)]
-        w_scales = [tile("w_scales%d" % h, [P, NQ], U8) for h in range(H)]
+        w_words = [tile("w_words%d" % c, [P, QB * len(units)], U32) for c, units in enumerate(W_CALLS)]
+        w_scales = [tile("w_scales%d" % c, [P, QB * len(units)], U8) for c, units in enumerate(W_CALLS)]
         capped = [tile("capped%d" % g, [P, PACK, H, QB * n], F32) for g, (first, n) in enumerate(GROUPS)]
         u = [tile("u%d" % g, [P, PACK, H, QB * n], F32) for g, (first, n) in enumerate(GROUPS)]
-        warm = tile("warm", [P, 1], F32)
         denom, inverse, result = {}, {}, {}
 
         def blocks(first, n):
@@ -67,7 +72,7 @@ def tile_rows_a_relu2_kb_cap_kernel(tc, qT, kT, t, v, kb, out):
             return max(g for g, (first, n) in enumerate(GROUPS) if first <= block)
 
         def load_queries(g):
-            nc.sync.dma_start(out=q_raw[g][:], in_=qT.rearrange("h (p j) q -> (h p) j q", j=PACK)[:, :, blocks(*GROUPS[g])])
+            nc.sync.dma_start(out=q_raw[g][:], in_=qT.rearrange("h (p j) q -> (h p) j q", j=PACK)[:, :, blocks(g, 1)])
 
         def load_values(h):
             nc.sync.dma_start(out=v_raw[h][:], in_=v[h].rearrange("(p r) e -> p r e", r=PACK))
@@ -94,42 +99,42 @@ def tile_rows_a_relu2_kb_cap_kernel(tc, qT, kT, t, v, kb, out):
             nc.scalar.copy(out=views[0], in_=views[1])
 
         def quantise_queries(g):
-            cols = blocks(*GROUPS[g])
+            cols = blocks(g, 1)
             nc.vector.quantize_mx(out=q_words[:, cols].bitcast(FP8X4), scales=q_scales[:, cols],
                                   in_=q_bf[g][:].rearrange("p q j -> p (q j)"))
 
-        def round_values(h):
-            nc.vector.tensor_tensor(out=v_bf[:, h, :, :].rearrange("p (c i) r -> p c r i", i=RUN),
-                                    in0=v_raw[h][:].rearrange("p r (c i) -> p c r i", i=RUN),
-                                    in1=t_sign[:].unsqueeze(1).unsqueeze(3).to_broadcast([P, E // RUN, PACK, RUN]),
+        def round_values(h, part=slice(0, E)):
+            nc.vector.tensor_tensor(out=v_bf[:, h, part, :].rearrange("p (c i) r -> p c r i", i=RUN),
+                                    in0=v_raw[h][:, :, part].rearrange("p r (c i) -> p c r i", i=RUN),
+                                    in1=t_sign[:].unsqueeze(1).unsqueeze(3).to_broadcast([P, (part.stop - part.start) // RUN, PACK, RUN]),
                                     op=ALU.mult)
 
         def quantise_values(h):
             nc.vector.quantize_mx(out=v_words[:, h, :].bitcast(FP8X4), scales=v_scales[:, h, :],
                                   in_=v_bf[:, h, :, :].rearrange("p e r -> p (e r)"))
 
-        def score_view(step, h, first, n):
-            fill = [step in steps for steps in FILLS].index(True)
-            return score_bank[h][fill % SCORE_BANKS][:, blocks(FILLS[fill].index(step) + first, n)]
+        def score_view(g, r, h):
+            fill = [fg == g and r in tiles for fg, tiles in FILLS[h]].index(True)
+            n = GROUPS[g][1]
+            return score_bank[h][fill % SCORE_BANKS[h]][:, blocks(n * FILLS[h][fill][1].index(r), n)]
 
-        def scores(fill):
-            for h in range(H):
-                for step in FILLS[fill]:
-                    g, r = STEPS[step]
-                    first, n = GROUPS[g]
+        def scores(g, tiles, heads=range(H)):
+            first, n = GROUPS[g]
+            for h in heads:
+                for r in tiles:
                     for i in range(n):
                         cols = blocks(first + i, 1)
                         rows = slice(ROWS * h, ROWS * (h + 1))
-                        nc.tensor.matmul_mx(out=score_view(step, h, i, 1),
+                        nc.tensor.matmul_mx(out=score_view(g, r, h)[:, blocks(i, 1)],
                                             lhsT=k_words[rows, r, :].bitcast(FP8X4), lhsT_scale=k_scales[rows, r, :],
                                             rhs=q_words[rows, cols].bitcast(FP8X4), rhs_scale=q_scales[rows, cols],
                                             start=True, stop=True)
 
-        def cap(step, heads=range(H)):
-            g, r = STEPS[step]
+        def cap(g, tiles, heads=range(H)):
             for h in heads:
-                nc.scalar.activation(out=capped[g][:, r, h, :], in_=score_view(step, h, 0, GROUPS[g][1]),
-                                     func=ACT.Tanh, bias=kb_half[:, r : r + 1], scale=0.5)
+                for r in tiles:
+                    nc.scalar.activation(out=capped[g][:, r, h, :], in_=score_view(g, r, h),
+                                         func=ACT.Tanh, bias=kb_half[:, r : r + 1], scale=0.5)
 
         def relu_scale(g, r, heads=slice(0, H)):
             nc.vector.tensor_scalar(out=u[g][:, r, heads, :], in0=capped[g][:, r, heads, :], scalar1=0.0,
@@ -139,7 +144,8 @@ def tile_rows_a_relu2_kb_cap_kernel(tc, qT, kT, t, v, kb, out):
             g = group_of(block)
             first = QB * (block - GROUPS[g][0])
             src = u[g][:, :, h, first + part.start : first + part.stop].rearrange("p r (c i) -> p c r i", i=RUN)
-            dst = w_bf[h][:, QB * block + part.start : QB * block + part.stop, :].rearrange("p (c i) r -> p c r i", i=RUN)
+            call, place = place_of(W_CALLS, (block, h))
+            dst = w_bf[call][:, QB * place + part.start : QB * place + part.stop, :].rearrange("p (c i) r -> p c r i", i=RUN)
             return dst, src
 
         def square_on_vector(block, h, part=range(QB)):
@@ -150,51 +156,46 @@ def tile_rows_a_relu2_kb_cap_kernel(tc, qT, kT, t, v, kb, out):
             dst, src = square_views(block, h, part)
             nc.scalar.activation(out=dst, in_=src, func=ACT.Square)
 
-        def quantise_weights(block, h, n=1):
-            cols = blocks(block, n)
-            nc.vector.quantize_mx(out=w_words[h][:, cols].bitcast(FP8X4), scales=w_scales[h][:, cols],
-                                  in_=w_bf[h][:, cols, :].rearrange("p q r -> p (q r)"))
+        def quantise_weights(call):
+            nc.vector.quantize_mx(out=w_words[call][:].bitcast(FP8X4), scales=w_scales[call][:],
+                                  in_=w_bf[call][:].rearrange("p q r -> p (q r)"))
 
-        def second_product(block, h, n=1):
-            for b in range(block, block + n):
-                bank, place = Y_PLACE[(b, h)]
+        def second_product(call):
+            for i, (block, h) in enumerate(W_CALLS[call]):
+                bank, place = place_of(Y_BANKS, (block, h))
                 nc.tensor.matmul_mx(out=y_bank[bank][:, place, :],
-                                    lhsT=w_words[h][:, blocks(b, 1)].bitcast(FP8X4), lhsT_scale=w_scales[h][:, blocks(b, 1)],
+                                    lhsT=w_words[call][:, blocks(i, 1)].bitcast(FP8X4), lhsT_scale=w_scales[call][:, blocks(i, 1)],
                                     rhs=v_words[:, h, :].bitcast(FP8X4), rhs_scale=v_scales[:, h, :],
                                     start=True, stop=True)
 
-        def y_view(block, h, n):
-            bank, place = Y_PLACE[(block, h)]
-            return y_bank[bank][:, place : place + n, :]
+        def denominator_on_vector(bank, first, n):
+            denom[bank, first] = tile("denom%d%d" % (bank, first), [P, n], F32)
+            nc.vector.tensor_scalar_add(out=denom[bank, first][:], in0=y_bank[bank][:, first : first + n, E - 1], scalar1=1.0)
 
-        def denominator_on_vector(block, h, n=1):
-            denom[(block, h)] = tile("denom%d%d" % (block, h), [P, n], F32)
-            nc.vector.tensor_scalar_add(out=denom[(block, h)][:], in0=y_view(block, h, n)[:, :, E - 1], scalar1=1.0)
+        def denominator_on_scalar(bank, first, n):
+            denom[bank, first] = tile("denom%d%d" % (bank, first), [P, n], F32)
+            nc.scalar.activation(out=denom[bank, first][:], in_=y_bank[bank][:, first : first + n, E - 1], func=ACT.Copy, bias=1.0)
 
-        def denominator_on_scalar(block, h, n=1):
-            denom[(block, h)] = tile("denom%d%d" % (block, h), [P, n], F32)
-            nc.scalar.activation(out=denom[(block, h)][:], in_=y_view(block, h, n)[:, :, E - 1], func=ACT.Copy, bias=1.0)
-
-        def invert(block, h, n=1):
-            inverse[(block, h)] = tile("inverse%d%d" % (block, h), [P, n], F32)
-            nc.vector.reciprocal(out=inverse[(block, h)][:], in_=denom[(block, h)][:])
-
-        def share_inverse(owner, block, h, first, n):
-            inverse[(block, h)] = inverse[owner][:, first : first + n]
-
-        def divide_on_vector(block, h, n=1):
-            result[(block, h)] = tile("result%d%d" % (block, h), [P, n, E], F32)
-            nc.vector.tensor_tensor(out=result[(block, h)][:], in0=y_view(block, h, n),
-                                    in1=inverse[(block, h)][:, 0:n].unsqueeze(2).to_broadcast([P, n, E]), op=ALU.mult)
-
-        def divide_on_scalar(block, h, n=1):
-            result[(block, h)] = tile("result%d%d" % (block, h), [P, n, E], F32)
+        def invert(bank, first, n):
+            inverted = tile("inverse%d%d" % (bank, first), [P, n], F32)
+            nc.vector.reciprocal(out=inverted[:], in_=denom[bank, first][:])
             for i in range(n):
-                nc.scalar.activation(out=result[(block, h)][:, i, :], in_=y_view(block, h, n)[:, i, :], func=ACT.Copy,
-                                     scale=inverse[(block, h)][:, i : i + 1])
+                inverse[bank, first + i] = inverted[:, i:n]
 
-        def store(block, h, n=1):
-            nc.sync.dma_start(out=out[h, blocks(block, n), :].rearrange("(b p) e -> p b e", p=P), in_=result[(block, h)][:])
+        def divide_on_vector(bank, first, n):
+            result[bank, first] = tile("result%d%d" % (bank, first), [P, n, E], F32)
+            nc.vector.tensor_tensor(out=result[bank, first][:], in0=y_bank[bank][:, first : first + n, :],
+                                    in1=inverse[bank, first][:, 0:n].unsqueeze(2).to_broadcast([P, n, E]), op=ALU.mult)
+
+        def divide_on_scalar(bank, first, n):
+            result[bank, first] = tile("result%d%d" % (bank, first), [P, n, E], F32)
+            for i in range(n):
+                nc.scalar.activation(out=result[bank, first][:, i, :], in_=y_bank[bank][:, first + i, :], func=ACT.Copy,
+                                     scale=inverse[bank, first + i][:, 0:1])
+
+        def store(bank, first, n=1, queue=nc.sync):
+            block, h = Y_BANKS[bank][first]
+            queue.dma_start(out=out[h, blocks(block, n), :].rearrange("(b p) e -> p b e", p=P), in_=result[bank, first][:])
 
         ctx.enter_context(tc.manual_schedule())
 
@@ -206,6 +207,7 @@ def tile_rows_a_relu2_kb_cap_kernel(tc, qT, kT, t, v, kb, out):
         load_queries(1)
         load_values(0)
         load_queries(2)
+        load_queries(3)
         load_values(1)
 
         nc.vector.scalar_tensor_tensor(out=t_abs[:], in0=t_raw[:], scalar=-1.0, in1=t_raw[:], op0=ALU.mult, op1=ALU.max)
@@ -228,87 +230,78 @@ def tile_rows_a_relu2_kb_cap_kernel(tc, qT, kT, t, v, kb, out):
         quantise_keys(3, 1)
         quantise_queries(1)
         round_values(0)
-        for step in range(SCORE_BANKS):
-            scores(step)
+        scores(0, [0, 1])
+        scores(0, [2, 3])
 
-        cap(0)
-        scores(3)
-        cap(1)
-        scores(4)
-        cap(2, [0])
-        cap(3, [0])
-        cap(2, [1])
-        cap(3, [1])
-        relu_scale(0, 0)
+        cap(0, [0, 1])
+        scores(1, [0, 1])
+        cap(0, [2, 3])
+        scores(1, [2, 3])
         round_on_vector(query_views(2))
-        relu_scale(0, 1)
-        relu_scale(0, 2)
+        relu_scale(0, 0)
+        round_on_vector(query_views(3))
         quantise_queries(2)
-        scores(5)
+        relu_scale(0, 1)
+        quantise_queries(3)
+        relu_scale(0, 2)
         relu_scale(0, 3)
         quantise_values(0)
 
-        cap(4, [0])
-        cap(5, [0])
-        cap(4, [1])
-        cap(5, [1])
-        scores(6)
-        cap(6, [0])
-        cap(7, [0])
-        cap(6, [1])
-        cap(7, [1])
-        scores(7)
+        cap(1, [0, 1])
+        scores(2, [0])
+        scores(2, [1])
+        cap(1, [2, 3])
+        scores(2, [2])
         for r in range(PACK):
             relu_scale(1, r)
         round_values(1)
         square_on_scalar(0, 0)
+        cap(2, [0], [0])
+        scores(2, [3])
+        cap(2, [1], [0])
+        cap(2, [0, 1], [1])
+        cap(2, [2, 3])
         square_on_vector(1, 0)
-        square_on_vector(0, 1)
-        quantise_weights(0, 0, n=2)
-
-        cap(8)
-        scores(8)
-        cap(9)
-        cap(10)
-        cap(11)
-        second_product(0, 0, n=2)
-        for r in range(PACK - 1):
-            relu_scale(2, r)
+        square_on_vector(1, 1)
+        quantise_weights(0)
+        second_product(0)
+        relu_scale(2, 0)
+        relu_scale(2, 1)
         for h in range(H):
-            relu_scale(2, PACK - 1, slice(h, h + 1))
+            for r in (2, 3):
+                relu_scale(2, r, slice(h, h + 1))
         quantise_values(1)
-        square_on_scalar(1, 1)
-        denominator_on_vector(0, 0, n=2)
-        quantise_weights(0, 1, n=2)
-        second_product(0, 1, n=2)
-        invert(0, 0, n=2)
+        square_on_scalar(0, 1)
+        denominator_on_scalar(0, 0, 2)
         square_on_scalar(2, 0)
-        square_on_vector(3, 0)
-        quantise_weights(2, 0)
-        square_on_vector(3, 1, range(64, QB))
-        denominator_on_vector(0, 1, n=2)
-        second_product(2, 0)
-        quantise_weights(3, 0)
-        second_product(3, 0)
-        invert(0, 1, n=2)
-        square_on_scalar(2, 1)
-        quantise_weights(2, 1)
-        square_on_scalar(3, 1, range(0, 64))
-        divide_on_scalar(0, 0, n=2)
+        square_on_scalar(3, 0)
+        square_on_scalar(3, 1, range(0, 80))
+        quantise_weights(1)
+        second_product(1)
+        invert(0, 0, 2)
+        square_on_vector(2, 1)
+        quantise_weights(2)
+        second_product(2)
+        square_on_vector(3, 1, range(80, QB))
+        quantise_weights(3)
+        second_product(3)
+        denominator_on_scalar(0, 2, 2)
+        divide_on_scalar(0, 0, 2)
         store(0, 0, n=2)
-        second_product(2, 1)
-        quantise_weights(3, 1)
-        second_product(3, 1)
-        denominator_on_scalar(2, 0, n=2)
-        divide_on_scalar(0, 1, n=2)
-        store(0, 1, n=2)
-        invert(2, 0, n=2)
-        denominator_on_vector(2, 1, n=2)
-        divide_on_scalar(2, 0, n=2)
-        store(2, 0, n=2)
-        invert(2, 1, n=2)
-        share_inverse((2, 1), 3, 1, 1, 1)
-        divide_on_vector(2, 1)
+        quantise_weights(4)
+        second_product(4)
+        quantise_weights(5)
+        second_product(5)
+        invert(0, 2, 2)
+        denominator_on_vector(1, 0, 2)
+        divide_on_scalar(0, 2, 2)
+        store(0, 2, n=2)
+        invert(1, 0, 2)
+        denominator_on_vector(2, 0, 2)
+        invert(2, 0, 2)
+        divide_on_scalar(1, 0, 2)
+        store(1, 0, n=2)
+        divide_on_vector(2, 0, 1)
+        store(2, 0)
+        divide_on_vector(2, 1, 1)
         store(2, 1)
-        divide_on_vector(3, 1)
-        store(3, 1)

@@ -49,11 +49,10 @@ def tile_rows_a_relu2_kb_cap_kernel(tc, qT, kT, t, v, kb, out):
             tile(name, [P, PACK], F32) for name in ("t_raw", "t_abs", "t_root", "t_sign", "kb_raw", "kb_half")]
 
         k_raw = [tile("k_raw%d" % m, [P, PACK, P // 2, PACK], F32) for m in range(2)]
-        q_raw = [tile("q_raw%d" % b, [P, PACK, QB], F32) for b in range(NQ // QB)]
+        q_raw = [tile("q_raw%d" % g, [P, PACK, QB * n], F32) for g, (first, n) in enumerate(GROUPS)]
         v_raw = [tile("v_raw%d" % h, [P, PACK, E], F32) for h in range(H)]
         k_bf = [tile("k_bf%d" % m, [P, PACK, P // 2, PACK], BF16) for m in range(2)]
-        warm = tile("warm", [P, 1], F32)
-        q_bf = [tile("q_bf%d" % b, [P, QB, PACK], BF16) for b in range(NQ // QB)]
+        q_bf = [tile("q_bf%d" % g, [P, QB * n, PACK], BF16) for g, (first, n) in enumerate(GROUPS)]
         v_bf = tile("v_bf", [P, H, E, PACK], BF16)
         w_bf = [tile("w_bf%d" % c, [P, QB * len(units), PACK], BF16) for c, units in enumerate(W_CALLS)]
         k_words, k_scales = tile("k_words", [P, PACK, P], U32), tile("k_scales", [P, PACK, P], U8)
@@ -72,7 +71,7 @@ def tile_rows_a_relu2_kb_cap_kernel(tc, qT, kT, t, v, kb, out):
             return max(g for g, (first, n) in enumerate(GROUPS) if first <= block)
 
         def load_queries(g):
-            nc.sync.dma_start(out=q_raw[g][:], in_=qT.rearrange("h (p j) q -> (h p) j q", j=PACK)[:, :, blocks(g, 1)])
+            nc.sync.dma_start(out=q_raw[g][:], in_=qT.rearrange("h (p j) q -> (h p) j q", j=PACK)[:, :, blocks(*GROUPS[g])])
 
         def load_values(h):
             nc.sync.dma_start(out=v_raw[h][:], in_=v[h].rearrange("(p r) e -> p r e", r=PACK))
@@ -99,7 +98,7 @@ def tile_rows_a_relu2_kb_cap_kernel(tc, qT, kT, t, v, kb, out):
             nc.scalar.copy(out=views[0], in_=views[1])
 
         def quantise_queries(g):
-            cols = blocks(g, 1)
+            cols = blocks(*GROUPS[g])
             nc.vector.quantize_mx(out=q_words[:, cols].bitcast(FP8X4), scales=q_scales[:, cols],
                                   in_=q_bf[g][:].rearrange("p q j -> p (q j)"))
 
@@ -207,13 +206,11 @@ def tile_rows_a_relu2_kb_cap_kernel(tc, qT, kT, t, v, kb, out):
         load_queries(1)
         load_values(0)
         load_queries(2)
-        load_queries(3)
         load_values(1)
 
         nc.vector.scalar_tensor_tensor(out=t_abs[:], in0=t_raw[:], scalar=-1.0, in1=t_raw[:], op0=ALU.mult, op1=ALU.max)
         nc.scalar.activation(out=t_root[:], in_=t_abs[:], func=ACT.Sqrt, scale=4.0)
         nc.scalar.activation(out=t_sign[:], in_=t_raw[:], func=ACT.Sign)
-        nc.scalar.activation(out=warm[:], in_=t_raw[:, 0:1], func=ACT.Tanh)
 
         round_on_vector(key_views(0))
         round_on_vector(query_views(0))
@@ -221,7 +218,7 @@ def tile_rows_a_relu2_kb_cap_kernel(tc, qT, kT, t, v, kb, out):
             quantise_keys(r, 0)
         quantise_queries(0)
         round_on_vector(key_views(1, slice(0, 2)))
-        round_on_scalar(key_views(1, slice(2, 4)))
+        round_on_vector(key_views(1, slice(2, 4)))
         nc.vector.tensor_scalar_mul(out=kb_half[:], in0=kb_raw[:], scalar1=0.5)
         quantise_keys(0, 1)
         quantise_keys(1, 1)
@@ -237,13 +234,11 @@ def tile_rows_a_relu2_kb_cap_kernel(tc, qT, kT, t, v, kb, out):
         scores(1, [0, 1])
         cap(0, [2, 3])
         scores(1, [2, 3])
-        round_on_vector(query_views(2))
         relu_scale(0, 0)
-        round_on_vector(query_views(3))
-        quantise_queries(2)
+        round_on_vector(query_views(2))
         relu_scale(0, 1)
-        quantise_queries(3)
         relu_scale(0, 2)
+        quantise_queries(2)
         relu_scale(0, 3)
         quantise_values(0)
 

@@ -24,7 +24,7 @@ GROUPS = [(0, 1), (1, 1), (2, 2)]
 FILLS = [[(0, [0]), (0, [1]), (0, [2, 3]), (1, [0, 1]), (1, [2, 3]), (2, [0]), (2, [1]), (2, [2]), (2, [3])],
          [(0, [0, 1]), (0, [2, 3]), (1, [0, 1]), (1, [2, 3]), (2, [0, 1]), (2, [2, 3])]]
 SCORE_BANKS = [3, 2]
-Y_BANKS = [[(0, 0), (1, 0), (0, 1), (1, 1)], [(2, 0), (3, 0)], [(2, 1), (3, 1)]]
+Y_BANKS = [[(0, 0), (1, 0), (2, 1), (3, 1)], [(0, 1), (1, 1)], [(2, 0), (3, 0)]]
 W_CALLS = [[(0, 0), (1, 0)], [(0, 1), (1, 1)], [(2, 0)], [(3, 0)], [(2, 1)], [(3, 1)]]
 
 
@@ -235,12 +235,12 @@ def tile_rows_a_relu2_kb_cap_kernel(tc, qT, kT, t, v, kb, out):
         cap(0, [2, 3])
         scores(1, [2, 3])
         relu_scale(0, 0)
-        round_on_vector(query_views(2))
-        relu_scale(0, 1)
-        relu_scale(0, 2)
-        quantise_queries(2)
-        relu_scale(0, 3)
         quantise_values(0)
+        relu_scale(0, 1)
+        round_on_vector(query_views(2))
+        relu_scale(0, 2)
+        relu_scale(0, 3)
+        quantise_queries(2)
 
         cap(1, [0, 1])
         scores(2, [0])
@@ -251,6 +251,7 @@ def tile_rows_a_relu2_kb_cap_kernel(tc, qT, kT, t, v, kb, out):
             relu_scale(1, r)
         round_values(1)
         square_on_scalar(0, 0)
+        square_on_scalar(0, 1, range(0, 32))
         cap(2, [0], [0])
         scores(2, [3])
         cap(2, [1], [0])
@@ -260,43 +261,43 @@ def tile_rows_a_relu2_kb_cap_kernel(tc, qT, kT, t, v, kb, out):
         square_on_vector(1, 1)
         quantise_weights(0)
         second_product(0)
+        quantise_values(1)
         relu_scale(2, 0)
         relu_scale(2, 1)
         for h in range(H):
             for r in (2, 3):
                 relu_scale(2, r, slice(h, h + 1))
-        quantise_values(1)
-        square_on_scalar(0, 1)
+        square_on_scalar(0, 1, range(32, QB))
         denominator_on_scalar(0, 0, 2)
-        square_on_scalar(2, 0)
         square_on_scalar(3, 0)
+        square_on_scalar(2, 1)
         square_on_scalar(3, 1, range(0, 80))
+        square_on_vector(2, 0)
         quantise_weights(1)
         second_product(1)
         invert(0, 0, 2)
-        square_on_vector(2, 1)
+        square_on_vector(3, 1, range(80, QB))
         quantise_weights(2)
         second_product(2)
-        square_on_vector(3, 1, range(80, QB))
         quantise_weights(3)
         second_product(3)
-        denominator_on_scalar(0, 2, 2)
         divide_on_scalar(0, 0, 2)
         store(0, 0, n=2)
+        denominator_on_scalar(1, 0, 2)
         quantise_weights(4)
         second_product(4)
         quantise_weights(5)
         second_product(5)
-        invert(0, 2, 2)
-        denominator_on_vector(1, 0, 2)
-        divide_on_scalar(0, 2, 2)
-        store(0, 2, n=2)
         invert(1, 0, 2)
         denominator_on_vector(2, 0, 2)
-        invert(2, 0, 2)
         divide_on_scalar(1, 0, 2)
         store(1, 0, n=2)
-        divide_on_vector(2, 0, 1)
-        store(2, 0)
-        divide_on_vector(2, 1, 1)
-        store(2, 1)
+        invert(2, 0, 2)
+        denominator_on_vector(0, 2, 2)
+        invert(0, 2, 2)
+        divide_on_scalar(2, 0, 2)
+        store(2, 0, n=2)
+        divide_on_vector(0, 2, 1)
+        store(0, 2)
+        divide_on_vector(0, 3, 1)
+        store(0, 3)

@@ -24,7 +24,7 @@ GROUPS = [(0, 1), (1, 1), (2, 2)]
 FILLS = [[(0, [0]), (0, [1]), (0, [2, 3]), (1, [0, 1]), (1, [2, 3]), (2, [0]), (2, [1]), (2, [2]), (2, [3])],
          [(0, [0, 1]), (0, [2, 3]), (1, [0, 1]), (1, [2, 3]), (2, [0, 1]), (2, [2, 3])]]
 SCORE_BANKS = [3, 2]
-Y_BANKS = [[(0, 0), (1, 0), (2, 1), (3, 1)], [(0, 1), (1, 1)], [(2, 0), (3, 0)]]
+Y_BANKS = [[(0, 0), (1, 0), (0, 1), (1, 1)], [(2, 0), (3, 0)], [(2, 1), (3, 1)]]
 W_CALLS = [[(0, 0), (1, 0)], [(0, 1), (1, 1)], [(2, 0)], [(3, 0)], [(2, 1)], [(3, 1)]]
 
 
@@ -256,48 +256,49 @@ def tile_rows_a_relu2_kb_cap_kernel(tc, qT, kT, t, v, kb, out):
         scores(2, [3])
         cap(2, [1], [0])
         cap(2, [0, 1], [1])
-        cap(2, [2, 3])
+        cap(2, [2, 3], [0])
+        square_on_scalar(0, 1, range(32, QB))
+        cap(2, [2, 3], [1])
         square_on_vector(1, 0)
         square_on_vector(1, 1)
         quantise_weights(0)
         second_product(0)
-        quantise_values(1)
         relu_scale(2, 0)
         relu_scale(2, 1)
-        for h in range(H):
-            for r in (2, 3):
-                relu_scale(2, r, slice(h, h + 1))
-        square_on_scalar(0, 1, range(32, QB))
-        denominator_on_scalar(0, 0, 2)
-        square_on_scalar(3, 0)
-        square_on_scalar(2, 1)
-        square_on_scalar(3, 1, range(0, 80))
-        square_on_vector(2, 0)
+        relu_scale(2, 2, slice(0, 1))
+        relu_scale(2, 3, slice(0, 1))
+        quantise_values(1)
         quantise_weights(1)
         second_product(1)
-        invert(0, 0, 2)
-        square_on_vector(3, 1, range(80, QB))
-        quantise_weights(2)
-        second_product(2)
+        relu_scale(2, 2, slice(1, 2))
+        relu_scale(2, 3, slice(1, 2))
+        square_on_scalar(3, 0)
+        square_on_scalar(2, 0, range(0, 32))
+        square_on_scalar(2, 1)
+        square_on_scalar(3, 1, range(0, 64))
+        square_on_vector(2, 0, range(32, QB))
         quantise_weights(3)
         second_product(3)
-        divide_on_scalar(0, 0, 2)
-        store(0, 0, n=2)
-        denominator_on_scalar(1, 0, 2)
+        denominator_on_vector(0, 0, 4)
+        quantise_weights(2)
+        second_product(2)
+        square_on_vector(3, 1, range(64, QB))
+        invert(0, 0, 4)
         quantise_weights(4)
         second_product(4)
         quantise_weights(5)
         second_product(5)
+        divide_on_scalar(0, 0, 2)
+        store(0, 0, n=2)
+        denominator_on_vector(1, 0, 2)
         invert(1, 0, 2)
+        divide_on_scalar(0, 2, 2)
+        store(0, 2, n=2)
         denominator_on_vector(2, 0, 2)
+        invert(2, 0, 2)
         divide_on_scalar(1, 0, 2)
         store(1, 0, n=2)
-        invert(2, 0, 2)
-        denominator_on_vector(0, 2, 2)
-        invert(0, 2, 2)
-        divide_on_scalar(2, 0, 2)
-        store(2, 0, n=2)
-        divide_on_vector(0, 2, 1)
-        store(0, 2)
-        divide_on_vector(0, 3, 1)
-        store(0, 3)
+        divide_on_vector(2, 0, 1)
+        store(2, 0)
+        divide_on_vector(2, 1, 1)
+        store(2, 1)

@@ -251,13 +251,13 @@ def tile_rows_a_relu2_kb_cap_kernel(tc, qT, kT, t, v, kb, out):
             relu_scale(1, r)
         round_values(1)
         square_on_scalar(0, 0)
-        square_on_scalar(0, 1, range(0, 32))
+        square_on_scalar(0, 1, range(0, 96))
         cap(2, [0], [0])
         scores(2, [3])
         cap(2, [1], [0])
         cap(2, [0, 1], [1])
         cap(2, [2, 3], [0])
-        square_on_scalar(0, 1, range(32, QB))
+        square_on_scalar(0, 1, range(96, QB))
         cap(2, [2, 3], [1])
         square_on_vector(1, 0)
         square_on_vector(1, 1)
@@ -275,17 +275,18 @@ def tile_rows_a_relu2_kb_cap_kernel(tc, qT, kT, t, v, kb, out):
         square_on_scalar(3, 0)
         square_on_scalar(2, 0, range(0, 32))
         square_on_scalar(2, 1)
-        square_on_scalar(3, 1, range(0, 64))
+        denominator_on_scalar(0, 0, 4)
+        square_on_scalar(3, 1, range(0, 48))
         square_on_vector(2, 0, range(32, QB))
         quantise_weights(3)
         second_product(3)
-        denominator_on_vector(0, 0, 4)
+        square_on_vector(3, 1, range(48, 88))
         quantise_weights(2)
         second_product(2)
-        square_on_vector(3, 1, range(64, QB))
-        invert(0, 0, 4)
+        square_on_vector(3, 1, range(88, QB))
         quantise_weights(4)
         second_product(4)
+        invert(0, 0, 4)
         quantise_weights(5)
         second_product(5)
         divide_on_scalar(0, 0, 2)

@@ -208,12 +208,11 @@ def tile_rows_a_relu2_kb_cap_kernel(tc, qT, kT, t, v, kb, out):
         load_queries(2)
         load_values(1)
 
+        round_on_vector(key_views(0))
+        round_on_vector(query_views(0))
         nc.vector.scalar_tensor_tensor(out=t_abs[:], in0=t_raw[:], scalar=-1.0, in1=t_raw[:], op0=ALU.mult, op1=ALU.max)
         nc.scalar.activation(out=t_root[:], in_=t_abs[:], func=ACT.Sqrt, scale=4.0)
         nc.scalar.activation(out=t_sign[:], in_=t_raw[:], func=ACT.Sign)
-
-        round_on_vector(key_views(0))
-        round_on_vector(query_views(0))
         for r in range(PACK):
             quantise_keys(r, 0)
         quantise_queries(0)

from contextlib import ExitStack

import concourse.mybir as mybir

F32 = mybir.dt.float32
BF16 = mybir.dt.bfloat16
U32 = mybir.dt.uint32
U8 = mybir.dt.uint8
FP8X4 = mybir.dt.float8_e4m3fn_x4
ACT = mybir.ActivationFunctionType
ALU = mybir.AluOpType

H, D, NQ, N, E = 2, 256, 512, 512, 128
FLOPS = 2 * H * NQ * N * (D + E)

P = 128
PACK = 4
ROWS = D // PACK
QB = 128
HALF = N // 2
RUN = 4

GROUPS = [(0, 1), (1, 1), (2, 2)]
FILLS = [[(0, [0]), (0, [1]), (0, [2, 3]), (1, [0, 1]), (1, [2, 3]), (2, [0]), (2, [1]), (2, [2]), (2, [3])],
         [(0, [0, 1]), (0, [2, 3]), (1, [0, 1]), (1, [2, 3]), (2, [0, 1]), (2, [2, 3])]]
SCORE_BANKS = [3, 2]
Y_BANKS = [[(0, 0), (1, 0), (0, 1), (1, 1)], [(2, 0), (3, 0)], [(2, 1), (3, 1)]]
W_CALLS = [[(0, 0), (1, 0)], [(0, 1), (1, 1)], [(2, 0)], [(3, 0)], [(2, 1)], [(3, 1)]]


def place_of(rows, unit):
    row = [unit in units for units in rows].index(True)
    return row, rows[row].index(unit)


def tile_rows_a_relu2_kb_cap_kernel(tc, qT, kT, t, v, kb, out):
    nc = tc.nc
    with ExitStack() as ctx:
        sbuf = ctx.enter_context(tc.tile_pool(name="sbuf", bufs=1))
        psum = ctx.enter_context(tc.psum_pool(name="psum", bufs=1))

        def tile(name, shape, dtype):
            return sbuf.tile(shape, dtype, name=name, align_bytes=64)

        score_bank = [[psum.tile([P, 512], F32, name="score%d%d" % (h, b)) for b in range(SCORE_BANKS[h])] for h in range(H)]
        y_bank = [psum.tile([P, 4, E], F32, name="y%d" % b) for b in range(len(Y_BANKS))]

        t_raw, t_abs, t_root, t_sign, kb_raw, kb_half = [
            tile(name, [P, PACK], F32) for name in ("t_raw", "t_abs", "t_root", "t_sign", "kb_raw", "kb_half")]

        k_raw = [tile("k_raw%d" % m, [P, PACK, P // 2, PACK], F32) for m in range(2)]
        q_raw = [tile("q_raw%d" % g, [P, PACK, QB * n], F32) for g, (first, n) in enumerate(GROUPS)]
        v_raw = [tile("v_raw%d" % h, [P, PACK, E], F32) for h in range(H)]
        k_bf = [tile("k_bf%d" % m, [P, PACK, P // 2, PACK], BF16) for m in range(2)]
        q_bf = [tile("q_bf%d" % g, [P, QB * n, PACK], BF16) for g, (first, n) in enumerate(GROUPS)]
        v_bf = tile("v_bf", [P, H, E, PACK], BF16)
        w_bf = [tile("w_bf%d" % c, [P, QB * len(units), PACK], BF16) for c, units in enumerate(W_CALLS)]
        k_words, k_scales = tile("k_words", [P, PACK, P], U32), tile("k_scales", [P, PACK, P], U8)
        q_words, q_scales = tile("q_words", [P, NQ], U32), tile("q_scales", [P, NQ], U8)
        v_words, v_scales = tile("v_words", [P, H, E], U32), tile("v_scales", [P, H, E], U8)
        w_words = [tile("w_words%d" % c, [P, QB * len(units)], U32) for c, units in enumerate(W_CALLS)]
        w_scales = [tile("w_scales%d" % c, [P, QB * len(units)], U8) for c, units in enumerate(W_CALLS)]
        capped = [tile("capped%d" % g, [P, PACK, H, QB * n], F32) for g, (first, n) in enumerate(GROUPS)]
        u = [tile("u%d" % g, [P, PACK, H, QB * n], F32) for g, (first, n) in enumerate(GROUPS)]
        denom, inverse, result = {}, {}, {}

        def blocks(first, n):
            return slice(QB * first, QB * (first + n))

        def group_of(block):
            return max(g for g, (first, n) in enumerate(GROUPS) if first <= block)

        def load_queries(g):
            nc.sync.dma_start(out=q_raw[g][:], in_=qT.rearrange("h (p j) q -> (h p) j q", j=PACK)[:, :, blocks(*GROUPS[g])])

        def load_values(h):
            nc.sync.dma_start(out=v_raw[h][:], in_=v[h].rearrange("(p r) e -> p r e", r=PACK))

        def load_keys(m):
            nc.sync.dma_start(out=k_raw[m][:].rearrange("p j s r -> p j (s r)"),
                              in_=kT.rearrange("h (p j) i -> (h p) j i", j=PACK)[:, :, HALF * m : HALF * (m + 1)])

        def key_views(m, tiles=slice(0, PACK)):
            return k_bf[m][:, tiles, :, :].rearrange("p r s j -> p s j r"), k_raw[m][:, :, :, tiles].rearrange("p j s r -> p s j r")

        def quantise_keys(r, m):
            cols = slice(64 * m, 64 * (m + 1))
            nc.vector.quantize_mx(out=k_words[:, r, cols].bitcast(FP8X4), scales=k_scales[:, r, cols],
                                  in_=k_bf[m][:, r, :, :].rearrange("p s j -> p (s j)"))

        def query_views(g):
            return (q_bf[g][:].rearrange("p (c i) j -> p c j i", i=RUN), q_raw[g][:].rearrange("p j (c i) -> p c j i", i=RUN))

        def round_on_vector(views):
            nc.vector.tensor_copy(out=views[0], in_=views[1])

        def round_on_scalar(views):
            nc.scalar.copy(out=views[0], in_=views[1])

        def quantise_queries(g):
            cols = blocks(*GROUPS[g])
            nc.vector.quantize_mx(out=q_words[:, cols].bitcast(FP8X4), scales=q_scales[:, cols],
                                  in_=q_bf[g][:].rearrange("p q j -> p (q j)"))

        def round_values(h, part=slice(0, E)):
            nc.vector.tensor_tensor(out=v_bf[:, h, part, :].rearrange("p (c i) r -> p c r i", i=RUN),
                                    in0=v_raw[h][:, :, part].rearrange("p r (c i) -> p c r i", i=RUN),
                                    in1=t_sign[:].unsqueeze(1).unsqueeze(3).to_broadcast([P, (part.stop - part.start) // RUN, PACK, RUN]),
                                    op=ALU.mult)

        def quantise_values(h):
            nc.vector.quantize_mx(out=v_words[:, h, :].bitcast(FP8X4), scales=v_scales[:, h, :],
                                  in_=v_bf[:, h, :, :].rearrange("p e r -> p (e r)"))

        def score_view(g, r, h):
            fill = [fg == g and r in tiles for fg, tiles in FILLS[h]].index(True)
            n = GROUPS[g][1]
            return score_bank[h][fill % SCORE_BANKS[h]][:, blocks(n * FILLS[h][fill][1].index(r), n)]

        def scores(g, tiles, heads=range(H)):
            first, n = GROUPS[g]
            for h in heads:
                for r in tiles:
                    for i in range(n):
                        cols = blocks(first + i, 1)
                        rows = slice(ROWS * h, ROWS * (h + 1))
                        nc.tensor.matmul_mx(out=score_view(g, r, h)[:, blocks(i, 1)],
                                            lhsT=k_words[rows, r, :].bitcast(FP8X4), lhsT_scale=k_scales[rows, r, :],
                                            rhs=q_words[rows, cols].bitcast(FP8X4), rhs_scale=q_scales[rows, cols],
                                            start=True, stop=True)

        def cap(g, tiles, heads=range(H)):
            for h in heads:
                for r in tiles:
                    nc.scalar.activation(out=capped[g][:, r, h, :], in_=score_view(g, r, h),
                                         func=ACT.Tanh, bias=kb_half[:, r : r + 1], scale=0.5)

        def relu_scale(g, r, heads=slice(0, H)):
            nc.vector.tensor_scalar(out=u[g][:, r, heads, :], in0=capped[g][:, r, heads, :], scalar1=0.0,
                                    scalar2=t_root[:, r : r + 1], op0=ALU.max, op1=ALU.mult)

        def square_views(block, h, part):
            g = group_of(block)
            first = QB * (block - GROUPS[g][0])
            src = u[g][:, :, h, first + part.start : first + part.stop].rearrange("p r (c i) -> p c r i", i=RUN)
            call, place = place_of(W_CALLS, (block, h))
            dst = w_bf[call][:, QB * place + part.start : QB * place + part.stop, :].rearrange("p (c i) r -> p c r i", i=RUN)
            return dst, src

        def square_on_vector(block, h, part=range(QB)):
            dst, src = square_views(block, h, part)
            nc.vector.tensor_tensor(out=dst, in0=src, in1=src, op=ALU.mult)

        def square_on_scalar(block, h, part=range(QB)):
            dst, src = square_views(block, h, part)
            nc.scalar.activation(out=dst, in_=src, func=ACT.Square)

        def quantise_weights(call):
            nc.vector.quantize_mx(out=w_words[call][:].bitcast(FP8X4), scales=w_scales[call][:],
                                  in_=w_bf[call][:].rearrange("p q r -> p (q r)"))

        def second_product(call):
            for i, (block, h) in enumerate(W_CALLS[call]):
                bank, place = place_of(Y_BANKS, (block, h))
                nc.tensor.matmul_mx(out=y_bank[bank][:, place, :],
                                    lhsT=w_words[call][:, blocks(i, 1)].bitcast(FP8X4), lhsT_scale=w_scales[call][:, blocks(i, 1)],
                                    rhs=v_words[:, h, :].bitcast(FP8X4), rhs_scale=v_scales[:, h, :],
                                    start=True, stop=True)

        def denominator_on_vector(bank, first, n):
            denom[bank, first] = tile("denom%d%d" % (bank, first), [P, n], F32)
            nc.vector.tensor_scalar_add(out=denom[bank, first][:], in0=y_bank[bank][:, first : first + n, E - 1], scalar1=1.0)

        def denominator_on_scalar(bank, first, n):
            denom[bank, first] = tile("denom%d%d" % (bank, first), [P, n], F32)
            nc.scalar.activation(out=denom[bank, first][:], in_=y_bank[bank][:, first : first + n, E - 1], func=ACT.Copy, bias=1.0)

        def invert(bank, first, n):
            inverted = tile("inverse%d%d" % (bank, first), [P, n], F32)
            nc.vector.reciprocal(out=inverted[:], in_=denom[bank, first][:])
            for i in range(n):
                inverse[bank, first + i] = inverted[:, i:n]

        def divide_on_vector(bank, first, n):
            result[bank, first] = tile("result%d%d" % (bank, first), [P, n, E], F32)
            nc.vector.tensor_tensor(out=result[bank, first][:], in0=y_bank[bank][:, first : first + n, :],
                                    in1=inverse[bank, first][:, 0:n].unsqueeze(2).to_broadcast([P, n, E]), op=ALU.mult)

        def divide_on_scalar(bank, first, n):
            result[bank, first] = tile("result%d%d" % (bank, first), [P, n, E], F32)
            for i in range(n):
                nc.scalar.activation(out=result[bank, first][:, i, :], in_=y_bank[bank][:, first + i, :], func=ACT.Copy,
                                     scale=inverse[bank, first + i][:, 0:1])

        def store(bank, first, n=1, queue=nc.sync):
            block, h = Y_BANKS[bank][first]
            queue.dma_start(out=out[h, blocks(block, n), :].rearrange("(b p) e -> p b e", p=P), in_=result[bank, first][:])

        ctx.enter_context(tc.manual_schedule())

        nc.scalar.dma_start(out=t_raw[:], in_=t.rearrange("(s r) o -> s (r o)", r=PACK))
        load_keys(0)
        load_queries(0)
        load_keys(1)
        nc.sync.dma_start(out=kb_raw[:], in_=kb.rearrange("(s r) o -> s (r o)", r=PACK))
        load_queries(1)
        load_values(0)
        load_queries(2)
        load_values(1)

        round_on_vector(key_views(0))
        round_on_vector(query_views(0))
        nc.vector.scalar_tensor_tensor(out=t_abs[:], in0=t_raw[:], scalar=-1.0, in1=t_raw[:], op0=ALU.mult, op1=ALU.max)
        nc.scalar.activation(out=t_root[:], in_=t_abs[:], func=ACT.Sqrt, scale=4.0)
        nc.scalar.activation(out=t_sign[:], in_=t_raw[:], func=ACT.Sign)
        for r in range(PACK):
            quantise_keys(r, 0)
        quantise_queries(0)
        round_on_vector(key_views(1, slice(0, 2)))
        round_on_vector(key_views(1, slice(2, 4)))
        nc.vector.tensor_scalar_mul(out=kb_half[:], in0=kb_raw[:], scalar1=0.5)
        quantise_keys(0, 1)
        quantise_keys(1, 1)
        round_on_vector(query_views(1))
        quantise_keys(2, 1)
        quantise_keys(3, 1)
        quantise_queries(1)
        round_values(0)
        scores(0, [0, 1])
        scores(0, [2, 3])

        cap(0, [0, 1])
        scores(1, [0, 1])
        cap(0, [2, 3])
        scores(1, [2, 3])
        relu_scale(0, 0)
        quantise_values(0)
        relu_scale(0, 1)
        round_on_vector(query_views(2))
        relu_scale(0, 2)
        relu_scale(0, 3)
        quantise_queries(2)

        cap(1, [0, 1])
        scores(2, [0])
        scores(2, [1])
        cap(1, [2, 3])
        scores(2, [2])
        for r in range(PACK):
            relu_scale(1, r)
        round_values(1)
        square_on_scalar(0, 0)
        square_on_scalar(0, 1, range(0, 96))
        cap(2, [0], [0])
        scores(2, [3])
        cap(2, [1], [0])
        cap(2, [0, 1], [1])
        cap(2, [2, 3], [0])
        square_on_scalar(0, 1, range(96, QB))
        cap(2, [2, 3], [1])
        square_on_vector(1, 0)
        square_on_vector(1, 1)
        quantise_weights(0)
        second_product(0)
        relu_scale(2, 0)
        relu_scale(2, 1)
        relu_scale(2, 2, slice(0, 1))
        relu_scale(2, 3, slice(0, 1))
        quantise_values(1)
        quantise_weights(1)
        second_product(1)
        relu_scale(2, 2, slice(1, 2))
        relu_scale(2, 3, slice(1, 2))
        square_on_scalar(3, 0)
        square_on_scalar(2, 0, range(0, 32))
        square_on_scalar(2, 1)
        denominator_on_scalar(0, 0, 4)
        square_on_scalar(3, 1, range(0, 48))
        square_on_vector(2, 0, range(32, QB))
        quantise_weights(3)
        second_product(3)
        square_on_vector(3, 1, range(48, 88))
        quantise_weights(2)
        second_product(2)
        square_on_vector(3, 1, range(88, QB))
        quantise_weights(4)
        second_product(4)
        invert(0, 0, 4)
        quantise_weights(5)
        second_product(5)
        divide_on_scalar(0, 0, 2)
        store(0, 0, n=2)
        denominator_on_vector(1, 0, 2)
        invert(1, 0, 2)
        divide_on_scalar(0, 2, 2)
        store(0, 2, n=2)
        denominator_on_vector(2, 0, 2)
        invert(2, 0, 2)
        divide_on_scalar(1, 0, 2)
        store(1, 0, n=2)
        divide_on_vector(2, 0, 1)
        store(2, 0)
        divide_on_vector(2, 1, 1)
        store(2, 1)
